import numpy as np, ml_dtypes
CORES = [1,5,17,21,33,37,49,53]
N = 8
BF = ml_dtypes.bfloat16
def gentries(a):
    return np.ascontiguousarray(a.reshape(8, 16, -1).transpose(0, 2, 1)).reshape(8, -1)
def gtable(e):
    e = np.asarray(e); return np.ascontiguousarray(e.reshape(8, -1, 16).transpose(0, 2, 1)).reshape(128, -1).astype(np.int32)
BASE, K, E, CL, RO = 4096, 1024, 2048, 3, 3
W = BASE + 2 * K
def injections(rng, share):
    v = np.argsort(rng.random((N, 8, W, 16), dtype=np.float32), axis=3)
    return np.where(rng.random((N, 8, W, 16), dtype=np.float32) < share, -1, v)
def parts(rng, v):
    return {"idm": v, "par": rng.integers(0, W, (N, 8, W)), "mnt": rng.integers(0, W, (N, 8, E)), "ac": rng.integers(0, E, (N, 8, 16, E)),
            "ns0": rng.integers(0, W, (N, 8, K)), "u0": rng.integers(0, 16, (N, 8, K)), "e0": rng.integers(0, E, (N, 8, K))}
def pack(d):
    return {"idm": np.ascontiguousarray(d["idm"].transpose(0, 1, 3, 2).reshape(N, 128, W)).astype(np.float32).astype(BF), "par": d["par"].astype(np.int32), "mnt": d["mnt"].astype(np.int32),
            "ac": np.ascontiguousarray(d["ac"].reshape(N, 128, E)).astype(np.int32), "ns0": np.stack([gtable(a) for a in d["ns0"]]), "u0": d["u0"].astype(np.int32), "e0": np.stack([gtable(a) for a in d["e0"]])}
def setup_inputs(rng):
    return pack(parts(rng, injections(rng, rng.choice(np.array([0.03125, 0.0625, 0.125, 0.25]), (N, 8, W, 1)))))
def skew(rng, hi, shape):
    v = np.minimum((hi * rng.random(shape) ** 3).astype(np.int64), hi - 1); s = rng.random(shape[:2] + (1,) * (len(shape) - 2)) < 0.5
    return np.where(s, v, hi - 1 - v)
def setup_inputs_spread(rng):
    return pack({"idm": injections(rng, 0.5 * rng.random((N, 8, W, 1)) ** 2), "par": skew(rng, W, (N, 8, W)), "mnt": skew(rng, W, (N, 8, E)), "ac": skew(rng, E, (N, 8, 16, E)),
                 "ns0": skew(rng, W, (N, 8, K)), "u0": skew(rng, 16, (N, 8, K)), "e0": skew(rng, E, (N, 8, K))})
def atends(rng, hi, shape):
    return np.where(rng.random(shape) < 0.8, (hi - 1) * rng.integers(0, 2, shape), rng.integers(0, hi, shape))
def setup_inputs_ends(rng):
    full = injections(rng, 0.0625); sp = np.full((N, 8, W, 16), -1); z = rng.random((N, 8, W)) < 0.75
    sp[..., 15] = np.where(z, 15, -1); sp[..., 0] = np.where(z, -1, 15)
    v = np.where(rng.random((N, 8, W, 1)) < 0.7, sp, full)
    mid = np.argsort(rng.random((N, 8, 2, 14)), axis=3) + 1
    v[:, :, [0, W - 1], 1:15] = np.where(rng.random(mid.shape) < 0.125, -1, mid); v[:, :, [0, W - 1], 0] = 0; v[:, :, [0, W - 1], 15] = 15
    d = {"idm": v, "par": atends(rng, W, (N, 8, W)), "mnt": atends(rng, W, (N, 8, E)), "ac": atends(rng, E, (N, 8, 16, E)),
         "ns0": atends(rng, W, (N, 8, K)), "u0": atends(rng, 16, (N, 8, K)), "e0": atends(rng, E, (N, 8, K))}
    d["par"][:, :, 0] = 0; d["par"][:, :, W - 1] = W - 1; d["mnt"][:, :, 0] = 0; d["mnt"][:, :, E - 1] = W - 1; d["ac"][:, :, 0, 0] = 0; d["ac"][:, :, 15, E - 1] = E - 1
    x = rng.random((N, 8, K)); top = x < 0.125; low = x > 0.875
    top[..., [1, 2, K - 1]] = True; low[..., [1, 2, K - 1]] = False; top[..., 0] = False; low[..., 0] = True
    for k, hi in (("ns0", W - 1), ("u0", 15), ("e0", E - 1)): d[k] = np.where(top, hi, np.where(low, 0, d[k]))
    return pack(d)
def setup_inputs_corners(rng):
    full = injections(rng, 0.0); v = np.where(rng.random(full.shape, dtype=np.float32) < 0.0625, -1, full); d = parts(rng, v); num = np.arange(W); row = np.arange(16)
    for r in range(N):
        for g in range(8):
            s = (g + 3 * r) % 8
            if s == 0:
                c = rng.integers(0, 3, (W, 1)); v[r, g] = np.where(c == 0, -1, np.where(c == 1, row, full[r, g]))
            if s == 1:
                one = row == rng.integers(0, 16, (W, 1)); v[r, g] = np.where(one | (rng.random((W, 1)) < 0.5), full[r, g], -1)
            if s in (2, 3, 4): v[r, g] = full[r, g]; d["par"][r, g] = (num, 0 * num, 0 * num + W - 1)[s - 2]
            if s == 5: d["par"][r, g] = np.maximum(num - 1, 0)
            if s == 6: d["par"][r, g] = rng.integers(BASE, W, W); d["mnt"][r, g] = rng.integers(BASE, W, E)
            if s == 7:
                hc = rng.permutation(BASE)[:64]; v[r, g, hc] = -1
                d["mnt"][r, g] = np.where((rng.random(E) < 0.0625) & (r % 2 == 0), d["mnt"][r, g], hc[rng.integers(0, 64, E)])
    z = rng.random((N, 8, K)); own = BASE + K * rng.integers(0, 2, (N, 8, K)) + np.arange(K); edge = rng.choice(np.array([0, W - 1, BASE - 1, BASE, BASE + K - 1, BASE + K]), (N, 8, K))
    d["ns0"] = np.where(z < 0.25, own, np.where(z < 0.5, edge, d["ns0"])); d["u0"] = np.where(rng.random((N, 8, K)) < 0.5, 15 * rng.integers(0, 2, (N, 8, K)), d["u0"])
    return pack(d)
def setup_inputs_alike(rng):
    d = parts(rng, injections(rng, 0.0625))
    for r in range(N):
        for g in range(8):
            s = (g + r) % 4
            for k, hi in (("ns0", W), ("e0", E)):
                old = d[k][r, g].copy(); few = rng.integers(0, hi, 4)
                if s < 2: d[k][r, g] = few[0]
                if s == 1: d[k][r, g, K - 1 - r] = old[K - 1 - r]
                if s == 2: d[k][r, g] = few[rng.integers(0, 4, K)]
            if s == 0: d["u0"][r, g] = rng.integers(0, 16)
        d["ac"][r, 2] = rng.integers(0, E); d["mnt"][r, 4] = rng.integers(0, W); d["par"][r, 6] = rng.integers(0, W)
    d["ac"][:, 1::2] = rng.choice(np.array([0, E - 1, E // 2, 3]), (N, 4, 16, E)); d["mnt"][:, 5] = rng.choice(np.array([0, W - 1, BASE, BASE + K]), (N, E))
    return pack(d)
def setup_inputs_calm(rng):
    v = (np.argsort(rng.random((N, 8, W, 4, 4), dtype=np.float32), axis=4) + 4 * np.arange(4)[:, None]).reshape(N, 8, W, 16)
    d = parts(rng, np.where(rng.random(v.shape, dtype=np.float32) < 0.05, -1, v))
    for g in range(8):
        h = (g + 1) % 8
        if g % 2 == 0:
            d["ns0"][:, g] = rng.integers(0, 4, (N, K)); d["u0"][:, g] = rng.integers(0, 4, (N, K)); d["e0"][:, g] = rng.integers(0, 4, (N, K)); d["par"][:, g] = rng.integers(0, 4, (N, W))
            d["ac"][:, h] = rng.integers(0, 4, (N, 16, E)); d["mnt"][:, h] = rng.choice(np.array([0, 1, 2, 3, BASE, BASE + 1, BASE + K, BASE + K + 1]), (N, E))
        else:
            d["ns0"][:, g] = W - 1 - rng.integers(0, 2, (N, K)); d["u0"][:, g] = 15 - rng.integers(0, 2, (N, K)); d["e0"][:, g] = E - 1 - rng.integers(0, 2, (N, K)); d["par"][:, g] = W - 1 - rng.integers(0, 2, (N, W))
            d["ac"][:, h] = E - 1 - rng.integers(0, 2, (N, 16, E)); d["mnt"][:, h] = rng.choice(np.array([W - 1, W - 2, BASE + K - 1, BASE + K - 2, BASE - 1, BASE - 2]), (N, E))
    return pack(d)
def check_inputs(d):
    bad = []
    for k, lo, hi in (("idm", -1, 15), ("par", 0, W - 1), ("mnt", 0, W - 1), ("ac", 0, E - 1), ("ns0", 0, W - 1), ("u0", 0, 15), ("e0", 0, E - 1)):
        v = np.asarray(d[k]).astype(np.float64)
        if not (np.min(v) >= lo and np.max(v) <= hi): bad.append("range of " + k)
    v = np.asarray(d["idm"]).astype(np.float32)
    if not np.all(v == np.rint(v)): bad.append("whole numbers in idm")
    s = np.sort(v.reshape(-1, 8, 16, W), axis=2)
    if np.any((s[:, :, 1:] == s[:, :, :-1]) & (s[:, :, 1:] >= 0)): bad.append("an id twice in a column of idm")
    return bad
def reference(idm, par, mnt, ac, ns0, u0, e0):
    a = np.ascontiguousarray(idm.astype(np.float32).astype(np.int64).reshape(N, 8, 16, W).transpose(0, 1, 3, 2))
    p = par.astype(np.int64); mt = mnt.astype(np.int64); mv = ac.astype(np.int64).reshape(N, 8, 16, E)
    ns = np.stack([gentries(x) for x in ns0]).astype(np.int64); e = np.stack([gentries(x) for x in e0]).astype(np.int64); u = u0.astype(np.int64)
    R = np.arange(N)[:, None, None]; G = np.arange(8)[None, :, None]; H = (G + 1) % 8
    for t in range(RO):
        w = u; n = ns
        for step in range(CL):
            w = np.where(w >= 0, a[R, G, n, np.maximum(w, 0)], -1); n = p[R, G, n]
        Q = (R + 1 + t % (N - 1)) % N
        col = a[Q, H, mt[Q, H, e]]
        hit = (col == w[..., None]) & (w[..., None] >= 0); ok = np.any(hit, axis=3); k = np.argmax(hit, axis=3)
        e2 = mv[Q, H, k, e]; up = p[R, G, ns]; S = BASE + K * (t % 2)
        if t < RO - 1:
            a[:, :, S:S + K] = np.where(ok[..., None], col, a[:, :, S:S + K]); p[:, :, S:S + K] = np.where(ok, ns, p[:, :, S:S + K])
        ns = np.where(ok, S + e2 % K, up); u = np.where(ok, k, u); e = np.where(ok, e2, e)
    return {"yn": np.stack([gtable(x) for x in ns]).astype(np.float32), "yu": u.astype(np.float32), "ye": np.stack([gtable(x) for x in e]).astype(np.float32)}

@@ -1,0 +1,513 @@
+import numpy as np
+from concourse.bass import DstId, RemoteDMATransfer
+from concourse.mybir import dt, AluOpType, AxisListType, ActivationFunctionType
+
+N, BASE, K, E, W, RO = 8, 4096, 1024, 2048, 6144, 3
+H = 512
+NCH = 6
+CONV = "aaavvv"
+ALU = AluOpType
+ACT = ActivationFunctionType
+
+
+def sb(n, d, p=128):
+    return ("sbuf", [p, n], d)
+
+
+SCRATCH = {
+    "A": sb(W, "bfloat16"), "PT": sb(W, "bfloat16"), "AC": sb(E, "int32"),
+    "DEN": sb(512, "int32"), "DHI": sb(512, "bfloat16"), "DLO": sb(512, "bfloat16"),
+    "EI": sb(64, "int32"), "NI": sb(64, "int32"), "UI": sb(64, "int32"),
+    "UB": sb(64, "bfloat16"), "IDW": sb(132, "bfloat16"), "U8": sb(K, "bfloat16", 8),
+    "XMI": sb(176, "int32"), "XM": sb(176, "int32"), "XB": sb(160, "int32"),
+    "KI": sb(8, "int32"), "C": sb(24, "float32"), "ERI": sb(64, "int32"),
+    "MV": sb(128, "bfloat16"), "SG": sb(128, "bfloat16"), "WP": sb(128, "bfloat16"),
+    "Y": sb(144, "bfloat16"), "YN": sb(144, "bfloat16"), "I64": sb(128, "bfloat16"), "SH": sb(128, "float16"),
+    "WZ1": sb(128, "bfloat16"), "WZ2": sb(128, "bfloat16"), "WZ": sb(128, "bfloat16"), "SEL": sb(128, "bfloat16", 8),
+    "EP": sb(144, "bfloat16"), "EM": sb(144, "bfloat16"), "EV": sb(144, "float16"), "EK": sb(3 * 144, "bfloat16"),
+    "ONES": sb(576, "bfloat16"), "MA": sb(16 * 144, "bfloat16"), "IWR": sb(64, "float32"), "XW": sb(256, "float32"),
+    "EU": sb(3 * 64, "uint16"), "ER": sb(3 * 64, "uint16"), "NO": sb(128, "uint16"), "N1U": sb(64, "uint16"),
+    "N2U": sb(64, "uint16"), "MU": sb(64, "uint16"),
+    "E1": sb(64, "float32"), "NS": sb(64, "float32"), "UPS": sb(64, "float32"),
+    "U": sb(64, "float32"), "UJ": sb(64, "int32"), "UK": sb(64, "int32"), "UF": sb(64, "float32"), "EF": sb(64, "float32"),
+    "NOK": sb(64, "float32"), "TE": sb(64, "float32"), "TB": sb(64, "float32"), "TN": sb(128, "float32"),
+    "TD": sb(128, "float32"), "PH": sb(64, "bfloat16"), "PL": sb(64, "bfloat16"),
+    "PG": sb(K, "bfloat16"), "PG2": sb(K, "bfloat16"), "MG": sb(K, "bfloat16"),
+    "Z0": sb(K, "bfloat16"), "Z1": sb(K, "bfloat16"), "Z2": sb(K, "bfloat16"), "TT": sb(K, "bfloat16"),
+    "HIT": sb(K, "bfloat16"), "VAL": sb(K, "float16"),
+    "CS": sb(3 * K, "bfloat16"), "CL": sb(3 * K, "bfloat16"), "AS": sb(3 * K, "float16"), "AL": sb(3 * K, "float16"),
+    "WIN": sb(4 * K, "bfloat16"),
+    "S0": ("psum", [128, 512], "float32"), "S1": ("psum", [128, 512], "float32"),
+    "ZB0": ("psum", [128, 512], "float32"), "ZB1": ("psum", [128, 512], "float32"),
+    "AB0": ("psum", [128, 512], "float32"), "AB1": ("psum", [128, 512], "float32"),
+    "X0": ("psum", [128, 512], "float32"), "X1": ("psum", [128, 512], "float32"),
+}
+BANKS = [k for k, v in SCRATCH.items() if v[0] == "psum"]
+DMAS = (["le", "lp", "lu", "lu8", "lpt", "lac", "oe", "on", "ou"] + ["li%d" % i for i in range(NCH)]
+        + ["sh%d%d" % (t, h) for t in range(2) for h in range(2)])
+ARR = (["re00"] + ["re%d%d" % (t, h) for t in (1, 2) for h in range(2)]
+       + ["r%s%d%d" % (x, t, h) for x in "ca" for t in range(3) for h in range(2)])
+SEMAPHORES = ["cv", "ca", "cp", "cg", "loc"] + DMAS + ARR
+
+CK, CG16, CR, CM01, CM14, CB1, CB961, CBU, CK16, CKT = 0, 1, 2, 3, 4, 5, 6, 7, 8, 9
+CW1, CW, CQ1, CQ2, CQ3, CBP = 13, 14, 15, 16, 17, 18
+OPT = {"ins": "av", "mg": "aa", "cg": "aa", "pg0": "av", "pg1": "aa", "xm": 2, "x1": 1, "x2": 2,
+       "sn": "a", "ph": "a", "ns": "a", "nl": "v", "ef": "a", "cv": "aaaavv"}
+
+CYC, GAT, PEC, FIX, SEM = 1.04e-3, 1.56, 0.55e-3, 0.04, 0.12
+DFIX, DRATE, RFIX, RRATE = 1.8, 260e3, 2.4, 80e3
+
+
+def build_ops(g, T, topo, core):
+    ops = []
+    rank = T.rank_of(core)
+    V, S, P = g.vector, g.scalar, g.tensor
+
+    def add(name, q, fn, r, w, dur, kind="c", extra=None):
+        ops.append({"name": name, "q": q, "fn": fn, "r": r, "w": w, "dur": dur, "kind": kind, "x": extra})
+
+    def ts(name, out, in0, s1, s2, op0, op1, r, w, n, f=1.0):
+        if op1 is None:
+            add(name, "v", lambda: [V.tensor_scalar(out, in0, s1, None, op0)], r, w, FIX + max(n * f, 64) * CYC)
+        else:
+            add(name, "v", lambda: [V.tensor_scalar(out, in0, s1, s2, op0, op1)], r, w, FIX + max(n * f, 64) * CYC)
+
+    def tt(name, out, in0, in1, op, r, w, n, f=1.0):
+        add(name, "v", lambda: [V.tensor_tensor(out, in0, in1, op)], r, w, FIX + max(n * f, 64) * CYC)
+
+    def cp(name, out, in_, r, w, n, f=1.0):
+        add(name, "v", lambda: [V.tensor_copy(out, in_)], r, w, FIX + max(n * f, 64) * CYC)
+
+    def act(name, out, in_, func, bias, scale, r, w, n, f=1.0):
+        add(name, "a", lambda: [S.activation(out, in_, func, bias=bias, scale=scale)], r, w, FIX + max(n * f, 64) * CYC)
+
+    def pick(kind, h, name, out, in_, r, w):
+        if OPT[kind][h] == "v":
+            cp(name, out, in_, r, w, H, GAT)
+        else:
+            act(name, out, in_, ACT.Copy, 0.0, 1.0, r, w, H, GAT)
+
+    def mm(name, groups, r, w, cyc, opens=True, closes=True):
+        def fn():
+            last = []
+            for grp in groups:
+                for i, (o, l, x) in enumerate(grp):
+                    ins = P.matmul(o, l, x, opens and i == 0, closes and i == len(grp) - 1)
+                last.append(ins)
+            return last
+        add(name, "p", fn, r, w, FIX + cyc * PEC)
+
+    def dma(name, q, pairs, r, w, nbytes):
+        eng = g.sync if q == "s" else g.scalar
+        add(name, q, lambda: [eng.dma_start(o, i) for o, i in pairs], r, w, 0.1 * len(pairs), "d", nbytes)
+
+    def send(name, to_rank, from_rank, out, in_, r, w, nbytes):
+        dst, src = T.cores[to_rank % N], T.cores[from_rank % N]
+        rid, pid, _se = topo.addr(dst)
+
+        def fn():
+            g.remote_dma(out, in_, T.sem["r" + name], T.sem.loc, pid, rid, topo.mask(core, dst))
+            return []
+        add("s" + name, "g", fn, r, ["sent" + name], 0.3, "s", (nbytes, len(topo.engines(core, dst))))
+        add("r" + name, None, None, ["sent" + name], w, 0.0, "r", len(topo.engines(src, core)))
+
+    def col(j):
+        return T.C[:, j:j + 1]
+
+    def wide(h):
+        return slice(H * h, H * h + H)
+
+    def wr(h, o=0):
+        return slice(o + 32 * h, o + 32 * h + 32)
+
+    def extract(name, bank, weights, src, o, n, r, c0=0):
+        grp = [(T[bank][:, c0:c0 + n // 16], weights[:, 15 - a:143 - a], src[:, o + a:o + n:16]) for a in range(16)]
+        mm(name, [grp], r, [bank], 16 * 64)
+
+    AW = H
+    AK = ["A%d" % i for i in range(W // AW)]
+    PK = ["PTs", "PT00", "PT01", "PT10", "PT11"]
+
+    def ak(i):
+        return AK[i * len(AK) // NCH:(i + 1) * len(AK) // NCH]
+
+    dma("le", "s", [(T.EI[:], T.e0[:]), (T.NI[:], T.ns0[:])], [], ["EI", "NI"], 65536)
+    dma("lp", "s", [(T.DEN[:, 0:384], T.par[:]), (T.DEN[0:112, 384:512], T.mnt[1:8, :]),
+                    (T.DEN[112:128, 384:512], T.mnt[0:1, :])], [], ["DEN"], 262144)
+    dma("lu", "s", [(T.UK[:], T.u0[:])], [], ["UK"], 32768)
+    cp("ub", T.UB[:], T.UK[:], ["UK"], ["UB"], 64)
+    dma("lu8", "s", [(T.U8[:], T.UB[:])], ["UB"], ["U8"], 16384)
+    cw = W // NCH
+    for i in range(NCH):
+        dma("li%d" % i, "a", [(T.A[:, cw * i:cw * i + cw], T.idm[:, cw * i:cw * i + cw])], [], ak(i), 256 * cw)
+    add("fill", "v", lambda: [V.memset(T.PT[:], 0.0)], [], PK, FIX + W * 0.5 * CYC)
+    send("e00", rank + 1, rank - 1, T.ERI[:], T.EI[:], ["EI"], ["ERI"], 32768)
+    cp("er0", T.ER[:, 0:64], T.ERI[:], ["ERI"], ["ER00", "ER01"], 64)
+    cp("dhi", T.DHI[:], T.DEN[:], ["DEN"], ["DHI"], 512)
+    tt("dlo", T.DLO[:], T.DEN[:], T.DHI[:], ALU.subtract, ["DEN", "DHI"], ["DLO"], 512, 2)
+    dma("lpt", "s", [(T.PT[0:128:16, :], T.DHI[:, 0:384]), (T.PT[1:128:16, :], T.DLO[:, 0:384]),
+                     (T.PT[14:128:16, 0:E], T.DHI[:, 384:512]), (T.PT[15:128:16, 0:E], T.DLO[:, 384:512])],
+        ["DHI", "DLO"], PK + ["acgo"], 262144)
+    ops[-1]["early"] = True
+    dma("lac", "s", [(T.AC[0:112, :], T.ac[16:128, :]), (T.AC[112:128, :], T.ac[0:16, :])], [], ["AC"], 4 * 128 * E)
+    for i in range(NCH):
+        a = T.A[:, cw * i:cw * i + cw]
+        if OPT["cv"][i] == "a":
+            act("cv%d" % i, a, a, ACT.Identity, 1.0 / 64, 1.0 / 32, ak(i), ak(i), cw)
+        else:
+            ts("cv%d" % i, a, a, 0.5, 1.0 / 32, ALU.add, ALU.mult, ak(i), ak(i), cw, 0.5)
+    cp("nu0", T.NO[:, 0:64], T.NI[:], ["NI"], ["NU0", "NU1"], 64)
+    cp("ns0", T.NS[:], T.NI[:], ["NI"], ["NS0", "NS1"], 64)
+    ts("e10", T.E1[:], T.EI[:], 1.0, None, ALU.add, None, ["EI"], ["E10", "E11"], 64)
+
+    def gop(name, fn, r, w, n):
+        add(name, "g", lambda: [fn()], r, w, 0.17 + 2 * n * CYC)
+    gop("iki", lambda: g.iota(T.KI[:, 0:1], [[0, 1]], 0, 1), [], ["KI0"], 1)
+    gop("ixm", lambda: g.iota(T.XMI[:], [[1, 176]], 97, 0), [], ["XMI"], 176)
+    gop("iiw", lambda: g.iota(T.IWR[:], [[0, 2], [16, 32]], 0, 1, allow_small_or_imprecise_dtypes=True), [], ["IWR"], 64)
+    gop("ione", lambda: g.iota(T.ONES[:], [[0, 576]], 1, 0, allow_small_or_imprecise_dtypes=True), [], ["ONES"], 576)
+    for q in range(4):
+        gop("ma%d" % q, lambda q=q: g.affine_select(T.MA[:, 576 * q:576 * q + 576], T.ONES[:], [[-1, 4], [-16, 9], [1000, 16]],
+                                                    ALU.is_equal, 0.0, -1000 - 4 * q, 1), ["ONES"], ["MA%d" % q], 576)
+    gop("ick", lambda: g.iota(col(CK), [[0, 1]], 0, 1, allow_small_or_imprecise_dtypes=True), [], ["ck"], 1)
+    gop("ick16", lambda: g.iota(col(CK16), [[0, 1]], 0, 16, allow_small_or_imprecise_dtypes=True), [], ["ck16"], 1)
+    gop("idw", lambda: g.affine_select(T.IDW[:], T.ONES[:, 0:132], [[-1, 132]], ALU.is_equal, 0.0, 3, 1), ["ONES"], ["IDW"], 132)
+    ts("kg", T.KI[:, 4:5], T.KI[:, 0:1], 112, None, ALU.bitwise_and, None, ["KI0"], ["KI1"], 1)
+    ts("kr", T.KI[:, 5:6], T.KI[:, 0:1], 15, None, ALU.bitwise_and, None, ["KI0"], ["KI2"], 1)
+    cp("cr", T.C[:, CG16:CG16 + 2], T.KI[:, 4:6], ["KI1", "KI2"], ["cr", "cg"], 1)
+    ts("cm14", col(CM14), col(CR), 13.5, None, ALU.is_ge, None, ["cr"], ["cm14"], 1)
+    ts("cb1", col(CB1), col(CR), -2.0, -1.0, ALU.mult, ALU.add, ["cr"], ["cb1"], 1)
+    ts("cb961", col(CB961), col(CR), -2.0, -961.0, ALU.mult, ALU.add, ["cr"], ["cb961"], 1)
+    ts("cbu", col(CBU), col(CR), -2.0, None, ALU.mult, None, ["cr"], ["cbu"], 1)
+    ts("xm", T.XM[:], T.XMI[:], 127, None, ALU.bitwise_and, None, ["XMI"], ["XM"], 176)
+    ts("xb", T.XB[:], T.XMI[:, 15:175], 112, None, ALU.bitwise_and, None, ["XMI"], ["XB"], 160)
+    ts("sel", T.SEL[:], T.XB[0:8, 16:144], T.C[0:8, CK16:CK16 + 1], None, ALU.is_equal, None, ["XB", "ck16"], ["SEL"], 128)
+    ts("y", T.Y[:], T.XB[:, 0:144], col(CG16), None, ALU.is_equal, None, ["XB", "cg"], ["Y"], 144)
+    ts("yn", T.YN[:], T.XB[:, 0:144], col(CG16), -1.0, ALU.is_equal, ALU.mult, ["XB", "cg"], ["YN"], 144)
+    ts("cw1", col(CW1), col(CR), 2.0, -2.0, ALU.is_equal, ALU.mult, ["cr"], ["cw1"], 1)
+    ts("cw", col(CW), col(CR), 4.5, col(CW1), ALU.is_lt, ALU.add, ["cr", "cw1"], ["cw"], 1)
+    ts("cq1", col(CQ1), col(CR), -3.0, col(CR), ALU.add, ALU.mult, ["cr"], ["cq1"], 1)
+    ts("cq2", col(CQ2), col(CQ1), 0.0, 16.0, ALU.not_equal, ALU.mult, ["cq1"], ["cq2"], 1)
+    ts("cq3", col(CQ3), col(CR), -2.0, 0.0, ALU.add, ALU.min, ["cr"], ["cq3"], 1)
+    ts("cbp", col(CBP), col(CQ3), 8192.0, col(CQ2), ALU.mult, ALU.add, ["cq3", "cq2"], ["cbp"], 1)
+    ts("ep", T.EP[:, 0:143], T.XM[:, 16:159], col(CG16), col(CW), ALU.is_equal, ALU.mult, ["XM", "cg", "cw"], ["EP"], 143)
+    gop("isg", lambda: g.iota(T.SG[:], [[0, 8], [-4096, 16]], 8192, 0, allow_small_or_imprecise_dtypes=True), [], ["SG"], 128)
+    ts("em", T.EM[:, 0:143], T.XM[:, 0:143], col(CG16), col(CM14), ALU.is_equal, ALU.mult, ["XM", "cg", "cm14"], ["EM"], 143)
+    ts("ev", T.EV[:, 0:143], T.XM[:, 32:175], col(CG16), None, ALU.is_equal, None, ["XM", "cg"], ["EV"], 143)
+    ts("ckt", col(CKT), col(CR), 16.0, None, ALU.add, None, ["cr"], ["ckt"], 1)
+    ts("ek", T.EK[:, 0:143], T.XM[:, 32:175], col(CG16), col(CKT), ALU.is_equal, ALU.mult, ["XM", "cg", "ckt"], ["EK"], 143)
+    ts("sh", T.SH[:], T.XM[:, 15:143], col(CK), None, ALU.is_equal, None, ["XM", "ck"], ["SH"], 128)
+    ts("wz2", T.WZ2[:], T.XB[:, 32:160], col(CG16), 2.0, ALU.is_equal, ALU.mult, ["XB", "cg"], ["WZ2"], 128)
+    gop("wz1", lambda: g.affine_select(T.WZ1[:], T.WZ2[:], [[1, 128]], ALU.not_equal, -62.0, 16, -1), ["WZ2"], ["WZ1"], 128)
+    gop("wz", lambda: g.affine_select(T.WZ[:], T.WZ1[:], [[1, 128]], ALU.not_equal, -62.0, -112, -1), ["WZ1"], ["WZ"], 128)
+    tt("wp", T.WP[:], T.SG[:], T.WZ2[:], ALU.mult, ["SG", "WZ2"], ["WP"], 128, 2)
+    for t in range(2):
+        ts("iw%d" % t, T.XW[:, 128 * t + 64:128 * t + 128], T.IWR[:], col(CG16), float(1 - BASE - K * t), ALU.subtract, ALU.add,
+           ["IWR", "cg"], ["IW%d" % t], 64)
+
+    for h in range(2):
+        mm("pu%d" % h, [[(T["S%d" % h][:], T.SEL[:], T.U8[:, wide(h)])]], ["SEL", "U8"], ["S%d" % h], H)
+        act("z0i%d" % h, T.Z0[:, wide(h)], T["S%d" % h][:], ACT.Abs, col(CBU), 2.0, ["cbu"], ["S%d" % h, "Z0%d" % h], H)
+
+    def plus(kind, name, out, in_, c, r, w):
+        if OPT[kind] == "v":
+            ts(name, out, in_, c, None, ALU.add, None, r, w, 64)
+        else:
+            act(name, out, in_, ACT.Identity, c, 1.0, r, w, 64)
+
+    def lookup(name, parts, banks, weights, wk, src, sk, dst, dk, more=None):
+        for j in range(parts):
+            hs = [j] if parts == 2 else [0, 1]
+            n, nm, bank = H * len(hs), "%s%d" % (name, j), banks[j]
+            c = slice(32 * hs[0], 32 * hs[0] + 32 * len(hs))
+            extract("x" + nm, bank, weights, src, H * hs[0], n, [wk] + [sk + str(h) for h in hs])
+            cp("u" + nm, dst[:, c], T[bank][:, 0:n // 16], [], [bank] + [dk + str(h) for h in hs], 64)
+            if more is not None:
+                plus("sn", "s" + nm, T.UPS[:, c], T[bank][:, 0:n // 16], more, [], [bank] + ["UPS%d" % h for h in hs])
+
+    same, up1, nsame, nup1 = T.Y[:, 16:144], T.Y[:, 0:128], T.YN[:, 16:144], T.YN[:, 0:128]
+    for t in range(RO):
+        S0 = BASE + K * (t % 2)
+        last = t == RO - 1
+        n_ = lambda s, h=None, t=t: "%s_%d" % (s, t) if h is None else "%s_%d%d" % (s, t, h)
+        wino = 2 * K * t
+        for h in range(2):
+            er = T.ER[:, wr(h, 64 * t)]
+            erk = "ER%d%d" % (t, h)
+            pick("mg", h, n_("mg", h), T.MG[:, wide(h)], T.PT[:, 0:E].indirect(er), ["PTs", erk], ["MG%d" % h])
+        lookup(n_("m"), OPT["xm"], ("X1", "X1"), T.EM, "EM", T.MG, "MG", T.MU, "MU")
+        for h in range(2):
+            er = T.ER[:, wr(h, 64 * t)]
+            erk = "ER%d%d" % (t, h)
+            o = K * t + H * h
+            pick("cg", h, n_("cg", h), T.CS[:, o:o + H], T.A[:].indirect(T.MU[:, wr(h)]), AK + ["MU%d" % h], [n_("CS", h)])
+            send("c%d%d" % (t, h), rank - 1 - t, rank + 1 + t, T.CL[:, o:o + H], T.CS[:, o:o + H], [n_("CS", h)], [n_("CL", h)], 256 * H)
+            ts(n_("ag", h), T.AS[:, o:o + H], T.AC[:].indirect(er), 1.0, None, ALU.add, None, ["AC", erk], [n_("AS", h)], H, GAT)
+            send("a%d%d" % (t, h), rank - 1 - t, rank + 1 + t, T.AL[:, o:o + H], T.AS[:, o:o + H], [n_("AS", h)], [n_("AL", h)], 256 * H)
+        for h in range(2):
+            pick("pg0", h, n_("pg0", h), T.PG[:, wide(h)], T.PT[:].indirect(T.NO[:, wr(h)]), PK + ["NU%d" % h], ["PG%d" % h])
+        lookup(n_("n1"), OPT["x1"], ("X0", "AB1"), T.EP, "EP", T.PG, "PG", T.N1U, "N1U", float(1 - S0))
+        for h in range(2):
+            pick("pg1", h, n_("pg1", h), T.PG2[:, wide(h)], T.PT[:].indirect(T.N1U[:, wr(h)]), PK + ["N1U%d" % h], ["PG2%d" % h])
+        lookup(n_("n2"), OPT["x2"], ("AB0", "AB1"), T.EP, "EP", T.PG2, "PG2", T.N2U, "N2U")
+        if not last:
+            plus("ph", n_("ph"), T.PH[:], T.NS[:], 0.0, ["NS0", "NS1"], ["PH"])
+            tt(n_("pl"), T.PL[:], T.NS[:], T.PH[:], ALU.subtract, ["NS0", "NS1", "PH"], ["PL"], 64)
+            for h in range(2):
+                zb = "ZB%d" % h
+                for j in range(4):
+                    grp = [(T[zb][:], T.IDW[:, 0:128], T.PT[:, S0 + H * h:S0 + H * h + H])] if j == 0 else []
+                    for a in range(4 * j, 4 * j + 4):
+                        grp += [(T[zb][:, a:H:16], T.MA[:, 144 * a + 1:144 * a + 129], T.PH[:, wr(h)]),
+                                (T[zb][:, a:H:16], T.MA[:, 144 * a:144 * a + 128], T.PL[:, wr(h)])]
+                    mm(n_("pp%d" % j, h), [grp], ["IDW", "PT%d%d" % (t, h), "MA%d" % j, "PH", "PL"], [zb], 512 + (H if j == 0 else 0),
+                       j == 0, False)
+                wo, ao = wino + K * h + H, S0 + H * h
+                gop(n_("old", h), lambda wo=wo, ao=ao: g.affine_select(T.WIN[:, wo:wo + H], T.A[:, ao:ao + H], [[0, H]], ALU.is_equal, 0.0, 0, 0),
+                    ["A%d" % (ao // AW)], [n_("OLD", h)], H)
+        for h in range(2):
+            sbk, zb, ab, xb = "S%d" % h, "ZB%d" % h, "AB%d" % h, "X%d" % h
+            lists = (("NU", T.NO), ("N1U", T.N1U), ("N2U", T.N2U))
+            marks = (("Z0", T.Z0), ("Z1", T.Z1), ("Z2", T.Z2))
+            tk, ttv = "TT%d" % h, T.TT[:, wide(h)]
+            for s in range(3):
+                zk, z = marks[s][0] + str(h), marks[s][1][:, wide(h)]
+                tt(n_("g%d" % s, h), ttv, T.A[:].indirect(lists[s][1][:, wr(h)]), z, ALU.max,
+                   AK + [zk, lists[s][0] + str(h)], [tk], H, GAT)
+                pos, neg = (same, nsame) if s < 2 else (up1, nup1)
+                grp = [(T[sbk][:], pos, ttv)]
+                if s > 0 or t == 0:
+                    grp = [(T[sbk][:], neg, z)] + grp
+                mm(n_("ps%d" % s, h), [grp], ["Y", "YN", zk, tk], [sbk], H * len(grp))
+                if s < 2:
+                    bk, b = ("cb961", CB961) if (s == 0 and t > 0) else ("cb1", CB1)
+                    act(n_("z%d" % (s + 1), h), marks[s + 1][1][:, wide(h)], T[sbk][:], ACT.Abs, col(b), 64.0,
+                        [bk], [sbk, marks[s + 1][0] + str(h)], H)
+            o = K * t + H * h
+            hk, hv = "HIT%d" % h, T.HIT[:, wide(h)]
+            tt(n_("hit", h), hv, T[sbk][:], T.CL[:, o:o + H], ALU.is_equal, [n_("CL", h)], [sbk, hk], H)
+            mm(n_("pa", h), [[(T[ab][:], T.SH[:], T.AL[:, o:o + H])]], ["SH", n_("AL", h)], [ab], H)
+            tt(n_("val", h), T.VAL[:, wide(h)], T[ab][:], hv, ALU.mult, [hk], [ab, "VAL%d" % h], H)
+            extract(n_("xv", h), "X0", T.EV, T.VAL, H * h, H, ["EV", "VAL%d" % h], 32 * h)
+            if not last:
+                dma("sh%d%d" % (t, h), "s", [(T.WIN[0:112, wino + K * h:wino + K * h + H], T.CL[16:128, o:o + H]),
+                                             (T.WIN[112:128, wino + K * h:wino + K * h + H], T.CL[0:16, o:o + H])],
+                    [n_("CL", h)], [n_("NEW", h)], 256 * H)
+                mm(n_("pq", h), [[(T[zb][:], T.WP[:], hv)]], ["WP", hk], [zb], H, False, True)
+                mm(n_("pz", h), [[(T[sbk][:], T.IDW[:, 3:131], T.Z0[:, wide(h)]), (T[sbk][:], T.WZ[:], hv)]],
+                   ["IDW", "WZ", "Z0%d" % h, hk], [sbk], 2 * H)
+                act(n_("z0", h), T.Z0[:, wide(h)], T[sbk][:], ACT.Sign, -0.5, 1.0, [], [sbk, "Z0%d" % h], H)
+            for hs in ([[h]] if not last else [[0, 1]] if h == 1 else []):
+                c = slice(32 * hs[0], 32 * hs[-1] + 32)
+                X = T.X0[:, c]
+                k_ = lambda s, hs=hs: [s + str(j) for j in hs]
+                ts(n_("nok", h), T.NOK[:, c], X, 0.0, None, ALU.is_equal, None, [], ["X0"] + k_("NOK"), 32)
+                tt(n_("te", h), T.TE[:, c], T.NOK[:, c], T.E1[:, c], ALU.mult, k_("NOK") + k_("E1"), k_("TE"), 32)
+                tt(n_("e1", h), T.E1[:, c], X, T.TE[:, c], ALU.add, k_("TE"), ["X0"] + k_("E1"), 32)
+                if last:
+                    plus("ef", n_("ef", h), T.EF[:], T.E1[:], -1.0, k_("E1"), k_("EF"))
+                    continue
+                euk = "EU%d%d" % (t + 1, h)
+                ts(n_("eu", h), T.EU[:, wr(h, 64 * t + 64)], T.E1[:, c], -1.0, None, ALU.add, None, k_("E1"), [euk], 32)
+                send("e%d%d" % (t + 1, h), rank + 2 + t, rank - 2 - t, T.ER[:, wr(h, 64 * t + 64)], T.EU[:, wr(h, 64 * t + 64)],
+                     [euk], ["ER%d%d" % (t + 1, h)], 8192)
+        xb, nw = T.XW[:, 128 * (t % 2):128 * (t % 2) + 64], (64 if last else 128)
+        ts(n_("tb"), T.TB[:], T.X0[:, 0:64], 1024.5, -1024.0, ALU.is_gt, ALU.mult, [], ["X0", "TB"], 64)
+        tt(n_("tn2"), xb, T.X0[:, 0:64], T.TB[:], ALU.add, ["TB"], ["X0", "TN2"], 64)
+        tt(n_("tn"), T.TN[:, 0:64], T.NOK[:], T.UPS[:], ALU.mult, ["NOK0", "NOK1", "UPS0", "UPS1"], ["TN"], 64)
+        if not last:
+            ts(n_("to"), T.TN[:, 64:128], T.X0[:, 0:64], 0.0, float(H), ALU.is_equal, ALU.mult, [], ["X0", "TO"], 64)
+        tt(n_("tn3"), T.TD[:, 0:nw], T.XW[:, 128 * (t % 2):128 * (t % 2) + nw], T.TN[:, 0:nw], ALU.add,
+           ["TN2", "TN", "TO", "IW%d" % (t % 2)], ["TD"], nw, 2 if nw > 64 else 1)
+        if not last:
+            ts(n_("nu"), T.NO[:], T.TD[:], float(S0 - 1), None, ALU.add, None, ["TD"], ["NU0", "NU1", "OU0", "OU1"], 128)
+        plus("nl" if last else "ns", n_("ns"), T.NS[:], T.TD[:, 0:64], float(S0 - 1), ["TD"], ["NS0", "NS1"])
+        kb = "S0" if last else "AB0"
+        grp = [(T[kb][:, 0:64], T.EK[:, 15 - a:143 - a], T.HIT[:, 64 * a:64 * a + 64]) for a in range(16)]
+        mm(n_("xk"), [grp], ["EK", "HIT0", "HIT1"], [kb], 1024)
+        tt(n_("u"), T.UJ[:], T[kb][:, 0:64], T.UK[:], ALU.max, ["UK"], [kb, "UJ"], 64)
+        ts(n_("uk"), T.UK[:], T.UJ[:], 15, None, ALU.bitwise_and, None, ["UJ"], ["UK"], 64)
+        if last:
+            cp("uf", T.UF[:], T.UK[:], ["UK"], ["UF"], 64)
+        if not last:
+            for h in range(2):
+                zb = "ZB%d" % h
+                a_out, a_in = T.A[:, S0 + H * h:S0 + H * h + H], T.WIN[:, wino + K * h:wino + K * h + K].indirect(T.NO[:, wr(h, 64)])
+                rk, wk = [n_("OLD", h), n_("NEW", h), "OU%d" % h], ["A%d" % ((S0 + H * h) // AW)]
+                pick("ins", h, n_("ins", h), a_out, a_in, rk, wk)
+                act(n_("pe", h), T.PT[:, S0 + H * h:S0 + H * h + H], T[zb][:], ACT.Relu, col(CBP), 1.0, ["cbp"], [zb, "PT%d%d" % (t, h)], H)
+    dma("oe", "s", [(T.ye[:], T.EF[:])], ["EF0", "EF1"], [], 32768)
+    dma("on", "a", [(T.yn[:], T.NS[:])], ["NS0", "NS1"], [], 32768)
+    dma("ou", "s", [(T.yu[:], T.UF[:])], ["UF"], [], 32768)
+    return ops
+
+
+def deps_of(ops):
+    lw, rd, out = {}, {}, []
+    for i, o in enumerate(ops):
+        d = set()
+        for k in o["r"]:
+            if k in lw:
+                d.add(lw[k])
+        look = [k for k in o["w"] if k in BANKS and o["q"] != "p"]
+        for k in o["w"]:
+            if k in lw:
+                d.add(lw[k])
+            d.update(j for j in rd.get(k, []) if k not in look or ops[j]["q"] != o["q"])
+        d.discard(i)
+        out.append(sorted(d))
+        for k in o["r"] + look:
+            rd.setdefault(k, []).append(i)
+        for k in o["w"]:
+            if k not in look:
+                lw[k] = i
+                rd[k] = []
+    return out
+
+
+def play(ops, deps, prio, gat=1.0, pe=1.0, net=1.0, order=None):
+    n = len(ops)
+    name = {o["name"]: i for i, o in enumerate(ops)}
+    succ = [[] for _ in ops]
+    left = [0] * n
+    for i in range(n):
+        pre = list(deps[i]) + ([name[ops[i]["after"]]] if "after" in ops[i] else [])
+        left[i] = len(pre)
+        for d in pre:
+            succ[d].append(i)
+    end, start, rdy = [0.0] * n, [0.0] * n, [0.0] * n
+    free = {"v": 0.0, "a": 0.0, "p": 0.0, "g": 0.0, "s": 0.0, "D": 0.0, "R": 0.0}
+    ready = [i for i in range(n) if left[i] == 0]
+    seq = []
+    pos = 0
+    first = [True]
+    while ready:
+        if order is not None:
+            i = order[pos]
+            pos += 1
+        else:
+            best = None
+            for j in ready:
+                q = ops[j]["q"]
+                st = rdy[j] if q is None else max(rdy[j], free[q])
+                key = (-1e9 if q is None else st - prio[j], j)
+                if best is None or key < best[0]:
+                    best = (key, j)
+            i = best[1]
+        ready.remove(i)
+        o = ops[i]
+        q = o["q"]
+        st = rdy[i] if q is None else max(rdy[i], free[q])
+        start[i] = st
+        dur = o["dur"]
+        if o["kind"] == "c":
+            if q == "p":
+                dur *= pe
+            elif dur > 0.8 and dur < 1.0 and q != "g":
+                dur *= gat
+            free[q] = end[i] = st + dur
+        elif o["kind"] == "d":
+            free[q] = st + dur
+            b = max(st + dur + DFIX * 0.7, free["D"])
+            free["D"] = b + o["x"] / DRATE * net
+            end[i] = free["D"] + DFIX * 0.3
+        elif o["kind"] == "s":
+            free[q] = st + dur + (1.0 if first[0] else 0.0)
+            first[0] = False
+            b = max(free[q] + RFIX * 0.6 * net, free["D"], free["R"])
+            free["R"] = b + o["x"][0] / RRATE * net
+            end[i] = free["R"] + RFIX * 0.4 * net
+        else:
+            end[i] = st
+        seq.append(i)
+        for j in succ[i]:
+            if ops[j].get("after") == o["name"] or (o["kind"] == "s" and ops[j]["kind"] != "r"):
+                t = free[q]
+            elif o["kind"] == "s" or (q == "p" and ops[j]["q"] == "p"):
+                t = end[i] if q != "p" else 0.0
+            else:
+                t = end[i] + SEM
+            rdy[j] = max(rdy[j], t)
+            left[j] -= 1
+            if left[j] == 0:
+                ready.append(j)
+    return seq, start, end
+
+
+MODELS = ((1.0, 1.0, 1.0), (0.7, 0.8, 0.8), (1.3, 1.0, 1.0), (1.0, 1.5, 1.3), (0.7, 1.0, 1.4))
+DIGITS = "0123456789abcdefghijklmnopqrstuvwxyzABCDEFGHIJKLMNOPQRSTUVWXYZ"
+ORDER = "0205010006070v0t0s0B0C0w0A0c0x0W0y0b0E0D0L0F030P0R0f0q0g0J0I0G0K0O0N0p0M0Q110Y0T0X120S0804090j0h0a0i1F0k0d181a0l1G0Z0V0n0e0r1v0o0m190H1R101b1c1u1d1M1N1e1w1f1S1g2d151h1x2e1O1H1I1i1l0u1j0z1T1U2f1o1z1J1V1K1B1W1A2g1r1C162h2i1y1m1p131s141X1n1D1Y1E172j201k1t1q2k1Z0U252122242m1P2l2728292a2n2q2o2p232r2G2t2z2u2B2A2C2v2D2K2M262s2b1L1Q2c2F2N3g2w2E2W2L3h2P2Q3i2J3s2x353j363t3n372T3u2y2O3O3P3k2R383a3Q2H3v3w322S3x2Z2X2U33302Y3R2V3b34313c3d3S3B3y3T393z3A3e3l3o3p3f3C3U3D3q3I3J3K2I3V3X3F3G3L3W3Y3M3m3r3E403N3Z414l3H4n444d454a464b4c474e4f4x4m4o424h4q4r4H48494k434G4u4I4R4J534D4p4S4s4t4T4L4y4z54554A4U4i564V4N4O4W574M584K4g4v4E4F4P4X4Y504j4Q595c5a4w4B4C4Z515b5d525o5e5p5q5r5j5f5k5l5g5m5h5n5u5i5t5s"
+PLAN = {}
+TRIES = 120
+
+
+def plan(ops, deps):
+    if ORDER:
+        seq = [DIGITS.index(ORDER[i]) * 62 + DIGITS.index(ORDER[i + 1]) for i in range(0, len(ORDER), 2)]
+        assert sorted(seq) == list(range(len(ops)))
+        place = {j: p for p, j in enumerate(seq)}
+        assert all(place[d] < place[i] for i in seq for d in deps[i])
+        return seq
+    if "seq" in PLAN:
+        return PLAN["seq"]
+    n = len(ops)
+    tail = [0.0] * n
+    for i in range(n - 1, -1, -1):
+        o = ops[i]
+        tail[i] += o["dur"] + SEM + (DFIX + o["x"] / DRATE if o["kind"] == "d" else RFIX + o["x"][0] / RRATE if o["kind"] == "s" else 0.0)
+        for d in deps[i]:
+            tail[d] = max(tail[d], tail[i])
+    rng = np.random.RandomState(1)
+    best = None
+    for k in range(TRIES):
+        wgt = (0.05, 0.1, 0.2, 0.4)[k % 4]
+        noise = rng.rand(n) * (0.0 if k < 4 else 0.3)
+        prio = [wgt * tail[i] + wgt * 4 * float(noise[i]) for i in range(n)]
+        seq, _s, _e = play(ops, deps, prio)
+        cost = sum(max(play(ops, deps, None, a, b, c, seq)[2]) for a, b, c in MODELS)
+        if best is None or cost < best[0]:
+            best = (cost, seq)
+    PLAN["seq"] = best[1]
+    PLAN["cost"] = best[0] / len(MODELS)
+    return best[1]
+
+
+def rank_program(g, core, T, topo):
+    if T.rank_of(core) is None:
+        return
+    ops = build_ops(g, T, topo, core)
+    deps = deps_of(ops)
+    seq = plan(ops, deps)
+    queue = {"v": g.vector, "a": g.scalar, "p": g.tensor, "g": g, "s": g.sync}
+    csem = {"v": "cv", "a": "ca", "p": "cp", "g": "cg"}
+    known = {q: {} for q in queue}
+    total = {}
+    mark = {}
+    for i in seq:
+        o = ops[i]
+        q = o["q"]
+        if o["kind"] == "r":
+            total[o["name"]] = o["x"]
+            mark[i] = (o["name"], o["x"], {})
+            continue
+        kn = known[q]
+        need = [mark[d] for d in deps[i] if d in mark and not (q == "p" and ops[d]["q"] == "p")]
+        for s, v, clock in sorted(need, key=lambda m: -m[1]):
+            if kn.get(s, 0) >= v:
+                continue
+            queue[q].wait_ge(T.sem[s], v)
+            kn[s] = v
+            for s2, v2 in clock.items():
+                kn[s2] = max(kn.get(s2, 0), v2)
+        ins = o["fn"]()
+        if o["kind"] == "s":
+            total["loc"] = total.get("loc", 0) + o["x"][1]
+            continue
+        s, step = (o["name"], 16) if o["kind"] == "d" else (csem[q], 1)
+        for x in ins:
+            x.then_inc(T.sem[s], step)
+            total[s] = total.get(s, 0) + step
+        mark[i] = (s, total[s], dict(kn))
+    for s, v in total.items():
+        if max(known[q].get(s, 0) for q in queue) < v:
+            g.wait_ge(T.sem[s], v)

@@ -1,11 +1,8 @@
-import numpy as np
-from concourse.bass import DstId, RemoteDMATransfer
-from concourse.mybir import dt, AluOpType, AxisListType, ActivationFunctionType
+from concourse.mybir import AluOpType, ActivationFunctionType
 
 N, BASE, K, E, W, RO = 8, 4096, 1024, 2048, 6144, 3
 H = 512
 NCH = 6
-CONV = "aaavvv"
 ALU = AluOpType
 ACT = ActivationFunctionType
 
@@ -17,45 +14,42 @@ def sb(n, d, p=128):
 SCRATCH = {
     "A": sb(W, "bfloat16"), "PT": sb(W, "bfloat16"), "AC": sb(E, "int32"),
     "DEN": sb(512, "int32"), "DHI": sb(512, "bfloat16"), "DLO": sb(512, "bfloat16"),
-    "EI": sb(64, "int32"), "NI": sb(64, "int32"), "UI": sb(64, "int32"),
+    "EI": sb(64, "int32"), "NI": sb(64, "int32"), "UK": sb(64, "int32"), "ERI": sb(64, "int32"),
     "UB": sb(64, "bfloat16"), "IDW": sb(132, "bfloat16"), "U8": sb(K, "bfloat16", 8),
-    "XMI": sb(176, "int32"), "XM": sb(176, "int32"), "XB": sb(160, "int32"),
-    "KI": sb(8, "int32"), "C": sb(24, "float32"), "ERI": sb(64, "int32"),
-    "MV": sb(128, "bfloat16"), "SG": sb(128, "bfloat16"), "WP": sb(128, "bfloat16"),
-    "Y": sb(144, "bfloat16"), "YN": sb(144, "bfloat16"), "I64": sb(128, "bfloat16"), "SH": sb(128, "float16"),
-    "WZ1": sb(128, "bfloat16"), "WZ2": sb(128, "bfloat16"), "WZ": sb(128, "bfloat16"), "SEL": sb(128, "bfloat16", 8),
-    "EP": sb(144, "bfloat16"), "EM": sb(144, "bfloat16"), "EV": sb(144, "float16"), "EK": sb(3 * 144, "bfloat16"),
-    "ONES": sb(576, "bfloat16"), "MA": sb(16 * 144, "bfloat16"), "IWR": sb(64, "float32"), "XW": sb(256, "float32"),
-    "EU": sb(3 * 64, "uint16"), "ER": sb(3 * 64, "uint16"), "NO": sb(128, "uint16"), "N1U": sb(64, "uint16"),
-    "N2U": sb(64, "uint16"), "MU": sb(64, "uint16"),
-    "E1": sb(64, "float32"), "NS": sb(64, "float32"), "UPS": sb(64, "float32"),
-    "U": sb(64, "float32"), "UJ": sb(64, "int32"), "UK": sb(64, "int32"), "UF": sb(64, "float32"), "EF": sb(64, "float32"),
-    "NOK": sb(64, "float32"), "TE": sb(64, "float32"), "TB": sb(64, "float32"), "TN": sb(128, "float32"),
-    "TD": sb(128, "float32"), "PH": sb(64, "bfloat16"), "PL": sb(64, "bfloat16"),
+    "XX": sb(256, "bfloat16"), "XB": sb(256, "bfloat16"), "KI": sb(8, "int32"), "C": sb(24, "float32"),
+    "SG": sb(128, "bfloat16"), "WP": sb(128, "bfloat16"), "Y": sb(256, "bfloat16"), "YN": sb(256, "bfloat16"),
+    "SH": sb(128, "float16"), "WZ1": sb(128, "bfloat16"), "WZ2": sb(128, "bfloat16"), "WZ": sb(128, "bfloat16"),
+    "SEL": sb(128, "bfloat16", 8), "EP": sb(144, "bfloat16"), "EM": sb(144, "bfloat16"), "EV": sb(144, "float16"),
+    "EK": sb(144, "bfloat16"), "EO": sb(144, "bfloat16"), "EF": sb(144, "bfloat16"),
+    "ONES": sb(576, "bfloat16"), "MA": sb(16 * 144, "bfloat16"), "IWR": sb(64, "float32"), "IW": sb(64, "float16"),
+    "EU": sb(3 * 64, "uint16"), "ER": sb(3 * 64, "uint16"), "NU": sb(64, "uint16"), "OU": sb(64, "uint16"),
+    "N1U": sb(64, "uint16"), "N2U": sb(64, "uint16"), "MU": sb(64, "uint16"),
+    "EY": sb(64, "int32"), "EN": sb(64, "int32"), "XI": sb(64, "int32"), "XL": sb(64, "int32"),
+    "NS": sb(64, "float32"), "UPS": sb(64, "float32"), "UO": sb(64, "float32"), "UJ": sb(64, "float32"),
+    "UF": sb(64, "float32"), "EW": sb(64, "float32"), "NOK": sb(64, "float32"), "TN": sb(64, "float32"),
+    "TD": sb(64, "float32"), "PH": sb(64, "bfloat16"), "PL": sb(64, "bfloat16"),
     "PG": sb(K, "bfloat16"), "PG2": sb(K, "bfloat16"), "MG": sb(K, "bfloat16"),
     "Z0": sb(K, "bfloat16"), "Z1": sb(K, "bfloat16"), "Z2": sb(K, "bfloat16"), "TT": sb(K, "bfloat16"),
     "HIT": sb(K, "bfloat16"), "VAL": sb(K, "float16"),
     "CS": sb(3 * K, "bfloat16"), "CL": sb(3 * K, "bfloat16"), "AS": sb(3 * K, "float16"), "AL": sb(3 * K, "float16"),
-    "WIN": sb(4 * K, "bfloat16"),
+    "WIN": sb(4 * K, "bfloat16"), "GC": sb(3 * K, "bfloat16"),
     "S0": ("psum", [128, 512], "float32"), "S1": ("psum", [128, 512], "float32"),
     "ZB0": ("psum", [128, 512], "float32"), "ZB1": ("psum", [128, 512], "float32"),
     "AB0": ("psum", [128, 512], "float32"), "AB1": ("psum", [128, 512], "float32"),
     "X0": ("psum", [128, 512], "float32"), "X1": ("psum", [128, 512], "float32"),
 }
 BANKS = [k for k, v in SCRATCH.items() if v[0] == "psum"]
-DMAS = (["le", "lp", "lu", "lu8", "lpt", "lac", "oe", "on", "ou"] + ["li%d" % i for i in range(NCH)]
+DMAS = (["le", "lp", "lu", "lu8", "lpt", "lac", "oe", "on", "ou", "old0", "old1"] + ["li%d" % i for i in range(NCH)]
         + ["sh%d%d" % (t, h) for t in range(2) for h in range(2)])
 ARR = (["re00"] + ["re%d%d" % (t, h) for t in (1, 2) for h in range(2)]
        + ["r%s%d%d" % (x, t, h) for x in "ca" for t in range(3) for h in range(2)])
-SEMAPHORES = ["cv", "ca", "cp", "cg", "loc"] + DMAS + ARR
+RELAYED = []
+SEMAPHORES = ["cv", "ca", "cp", "cg", "loc"] + DMAS + ARR + ["h" + n for n in RELAYED]
 
-CK, CG16, CR, CM01, CM14, CB1, CB961, CBU, CK16, CKT = 0, 1, 2, 3, 4, 5, 6, 7, 8, 9
-CW1, CW, CQ1, CQ2, CQ3, CBP = 13, 14, 15, 16, 17, 18
-OPT = {"ins": "av", "mg": "aa", "cg": "aa", "pg0": "av", "pg1": "aa", "xm": 2, "x1": 1, "x2": 2,
-       "sn": "a", "ph": "a", "ns": "a", "nl": "v", "ef": "a", "cv": "aaaavv"}
-
-CYC, GAT, PEC, FIX, SEM = 1.04e-3, 1.56, 0.55e-3, 0.04, 0.12
-DFIX, DRATE, RFIX, RRATE = 1.8, 260e3, 2.4, 80e3
+CK, CG16, CR, CM14, CB1, CB961, CBU, CKT, CRH, CW1, CW, CQ1, CQ2, CQ3, CBP = range(15)
+OPT = {"mg": "vaaaaa", "cg": "aaaaaa", "pg0": "aaavva", "pg1": "aaaaaa", "ins": "aaav", "hit": "vvvvvv", "cv": "aaavvv",
+       "g0": "ffffff", "g1": "ffffff", "g2": "ffffff", "n1": (("X0", "X0"), 64), "n2": (("X1", "X1"), 128),
+       "x1": "211", "x2": "222", "xm": "222", "xf": "22", "xv": "221", "lq": "ssssss"}
 
 
 def build_ops(g, T, topo, core):
@@ -63,53 +57,57 @@ def build_ops(g, T, topo, core):
     rank = T.rank_of(core)
     V, S, P = g.vector, g.scalar, g.tensor
 
-    def add(name, q, fn, r, w, dur, kind="c", extra=None):
-        ops.append({"name": name, "q": q, "fn": fn, "r": r, "w": w, "dur": dur, "kind": kind, "x": extra})
+    def add(name, q, fn, r, w, size, kind="c", extra=None):
+        ops.append({"name": name, "q": q, "fn": fn, "r": r, "w": w, "size": size, "kind": kind, "x": extra})
 
     def ts(name, out, in0, s1, s2, op0, op1, r, w, n, f=1.0):
         if op1 is None:
-            add(name, "v", lambda: [V.tensor_scalar(out, in0, s1, None, op0)], r, w, FIX + max(n * f, 64) * CYC)
+            add(name, "v", lambda: [V.tensor_scalar(out, in0, s1, None, op0)], r, w, (n, f))
         else:
-            add(name, "v", lambda: [V.tensor_scalar(out, in0, s1, s2, op0, op1)], r, w, FIX + max(n * f, 64) * CYC)
+            add(name, "v", lambda: [V.tensor_scalar(out, in0, s1, s2, op0, op1)], r, w, (n, f))
 
     def tt(name, out, in0, in1, op, r, w, n, f=1.0):
-        add(name, "v", lambda: [V.tensor_tensor(out, in0, in1, op)], r, w, FIX + max(n * f, 64) * CYC)
+        add(name, "v", lambda: [V.tensor_tensor(out, in0, in1, op)], r, w, (n, f))
 
     def cp(name, out, in_, r, w, n, f=1.0):
-        add(name, "v", lambda: [V.tensor_copy(out, in_)], r, w, FIX + max(n * f, 64) * CYC)
+        add(name, "v", lambda: [V.tensor_copy(out, in_)], r, w, (n, f))
 
     def act(name, out, in_, func, bias, scale, r, w, n, f=1.0):
-        add(name, "a", lambda: [S.activation(out, in_, func, bias=bias, scale=scale)], r, w, FIX + max(n * f, 64) * CYC)
+        add(name, "a", lambda: [S.activation(out, in_, func, bias=bias, scale=scale)], r, w, (n, f))
 
-    def pick(kind, h, name, out, in_, r, w):
-        if OPT[kind][h] == "v":
-            cp(name, out, in_, r, w, H, GAT)
+    def gop(name, fn, r, w, n):
+        add(name, "g", lambda: [fn()], r, w, (n, 2.0))
+
+    def pick(eng, name, out, in_, r, w):
+        if eng == "v":
+            cp(name, out, in_, r, w, H, "gather")
         else:
-            act(name, out, in_, ACT.Copy, 0.0, 1.0, r, w, H, GAT)
+            act(name, out, in_, ACT.Copy, 0.0, 1.0, r, w, H, "gather")
 
-    def mm(name, groups, r, w, cyc, opens=True, closes=True):
+    def mm(name, grp, r, w, cyc, opens=True, closes=True):
         def fn():
-            last = []
-            for grp in groups:
-                for i, (o, l, x) in enumerate(grp):
-                    ins = P.matmul(o, l, x, opens and i == 0, closes and i == len(grp) - 1)
-                last.append(ins)
-            return last
-        add(name, "p", fn, r, w, FIX + cyc * PEC)
+            for i, (o, l, x) in enumerate(grp):
+                ins = P.matmul(o, l, x, opens and i == 0, closes and i == len(grp) - 1)
+            return [ins]
+        add(name, "p", fn, r, w, (cyc, 1.0))
 
     def dma(name, q, pairs, r, w, nbytes):
         eng = g.sync if q == "s" else g.scalar
-        add(name, q, lambda: [eng.dma_start(o, i) for o, i in pairs], r, w, 0.1 * len(pairs), "d", nbytes)
+        add(name, q, lambda: [eng.dma_start(o, i) for o, i in pairs], r, w, (len(pairs), 1.0), "d", nbytes)
 
     def send(name, to_rank, from_rank, out, in_, r, w, nbytes):
-        dst, src = T.cores[to_rank % N], T.cores[from_rank % N]
+        dst, src, sem = T.cores[to_rank % N], T.cores[from_rank % N], "r" + name
+        engines = topo.engines(core, dst)
+        if name in RELAYED:
+            dst, src, sem = helper_of(core, T, topo), helper_of(src, T, topo), "h" + name
+            engines = [e for e in topo.engines(core, dst) if e not in engines]
         rid, pid, _se = topo.addr(dst)
 
         def fn():
-            g.remote_dma(out, in_, T.sem["r" + name], T.sem.loc, pid, rid, topo.mask(core, dst))
+            g.remote_dma(out, in_, T.sem[sem], T.sem.loc, pid, rid, sum(1 << e for e in engines))
             return []
-        add("s" + name, "g", fn, r, ["sent" + name], 0.3, "s", (nbytes, len(topo.engines(core, dst))))
-        add("r" + name, None, None, ["sent" + name], w, 0.0, "r", len(topo.engines(src, core)))
+        add("s" + name, "g", fn, r, ["sent" + name], (1, 1.0), "s", (nbytes, len(engines)))
+        add("r" + name, None, None, ["sent" + name], w, (0, 0.0), "r", len(topo.engines(src, core)))
 
     def col(j):
         return T.C[:, j:j + 1]
@@ -120,139 +118,141 @@ def build_ops(g, T, topo, core):
     def wr(h, o=0):
         return slice(o + 32 * h, o + 32 * h + 32)
 
-    def extract(name, bank, weights, src, o, n, r, c0=0):
-        grp = [(T[bank][:, c0:c0 + n // 16], weights[:, 15 - a:143 - a], src[:, o + a:o + n:16]) for a in range(16)]
-        mm(name, [grp], r, [bank], 16 * 64)
+    def cells(bank, c0, n):
+        return ["%s:%d" % (bank, c) for c in range(c0 // 32, (c0 + n) // 32)]
 
-    AW = H
-    AK = ["A%d" % i for i in range(W // AW)]
+    def extract(name, bank, weights, src, o, n, r, c0=0, more=()):
+        out = T[bank][:, c0:c0 + n // 16]
+        grp = [(out, l, x) for l, x in more] + [(out, weights[:, 15 - a:143 - a], src[:, o + a:o + n:16]) for a in range(16)]
+        mm(name, grp, r, cells(bank, c0, n // 16), len(grp) * 64)
+
+    def small(fn, *a):
+        return lambda: fn(*a, allow_small_or_imprecise_dtypes=True)
+
+    AK = ["A%d" % i for i in range(W // H)]
     PK = ["PTs", "PT00", "PT01", "PT10", "PT11"]
 
     def ak(i):
         return AK[i * len(AK) // NCH:(i + 1) * len(AK) // NCH]
 
-    dma("le", "s", [(T.EI[:], T.e0[:]), (T.NI[:], T.ns0[:])], [], ["EI", "NI"], 65536)
     dma("lp", "s", [(T.DEN[:, 0:384], T.par[:]), (T.DEN[0:112, 384:512], T.mnt[1:8, :]),
                     (T.DEN[112:128, 384:512], T.mnt[0:1, :])], [], ["DEN"], 262144)
+    dma("le", "s", [(T.EI[:], T.e0[:]), (T.NI[:], T.ns0[:])], [], ["EI", "NI"], 65536)
     dma("lu", "s", [(T.UK[:], T.u0[:])], [], ["UK"], 32768)
-    cp("ub", T.UB[:], T.UK[:], ["UK"], ["UB"], 64)
-    dma("lu8", "s", [(T.U8[:], T.UB[:])], ["UB"], ["U8"], 16384)
-    cw = W // NCH
-    for i in range(NCH):
-        dma("li%d" % i, "a", [(T.A[:, cw * i:cw * i + cw], T.idm[:, cw * i:cw * i + cw])], [], ak(i), 256 * cw)
-    add("fill", "v", lambda: [V.memset(T.PT[:], 0.0)], [], PK, FIX + W * 0.5 * CYC)
-    send("e00", rank + 1, rank - 1, T.ERI[:], T.EI[:], ["EI"], ["ERI"], 32768)
-    cp("er0", T.ER[:, 0:64], T.ERI[:], ["ERI"], ["ER00", "ER01"], 64)
+    add("fill0", "v", lambda: [V.memset(T.PT[:, 0:K], 0.0)], [], ["PTa"], (K, 0.5))
+    add("ones", "v", lambda: [V.memset(T.ONES[:], 1.0)], [], ["ONES"], (576, 0.5))
+    add("fill1", "v", lambda: [V.memset(T.PT[:, K:BASE], 0.0)], [], ["PTb"], (BASE - K, 0.5))
+    for t in range(2):
+        act("fill%d" % (2 + t), T.PT[:, BASE + K * t:BASE + K * t + K], T.PT[:, 0:K], ACT.Copy, 0.0, 1.0, ["PTa"],
+            ["PT%d0" % t, "PT%d1" % t], K)
     cp("dhi", T.DHI[:], T.DEN[:], ["DEN"], ["DHI"], 512)
     tt("dlo", T.DLO[:], T.DEN[:], T.DHI[:], ALU.subtract, ["DEN", "DHI"], ["DLO"], 512, 2)
+    cp("ub", T.UB[:], T.UK[:], ["UK"], ["UB"], 64)
+    dma("lu8", "s", [(T.U8[:], T.UB[:])], ["UB"], ["U8"], 16384)
     dma("lpt", "s", [(T.PT[0:128:16, :], T.DHI[:, 0:384]), (T.PT[1:128:16, :], T.DLO[:, 0:384]),
                      (T.PT[14:128:16, 0:E], T.DHI[:, 384:512]), (T.PT[15:128:16, 0:E], T.DLO[:, 384:512])],
-        ["DHI", "DLO"], PK + ["acgo"], 262144)
-    ops[-1]["early"] = True
+        ["DHI", "DLO"], PK + ["PTa", "PTb"], 262144)
+    cw = W // NCH
+    for i in range(NCH):
+        dma("li%d" % i, OPT["lq"][i], [(T.A[:, cw * i:cw * i + cw], T.idm[:, cw * i:cw * i + cw])], [], ak(i), 256 * cw)
     dma("lac", "s", [(T.AC[0:112, :], T.ac[16:128, :]), (T.AC[112:128, :], T.ac[0:16, :])], [], ["AC"], 4 * 128 * E)
+    send("e00", rank + 1, rank - 1, T.ERI[:], T.EI[:], ["EI"], ["ERI"], 32768)
+    cp("er0", T.ER[:, 0:64], T.ERI[:], ["ERI"], ["ER00", "ER01"], 64)
     for i in range(NCH):
         a = T.A[:, cw * i:cw * i + cw]
         if OPT["cv"][i] == "a":
             act("cv%d" % i, a, a, ACT.Identity, 1.0 / 64, 1.0 / 32, ak(i), ak(i), cw)
         else:
             ts("cv%d" % i, a, a, 0.5, 1.0 / 32, ALU.add, ALU.mult, ak(i), ak(i), cw, 0.5)
-    cp("nu0", T.NO[:, 0:64], T.NI[:], ["NI"], ["NU0", "NU1"], 64)
-    cp("ns0", T.NS[:], T.NI[:], ["NI"], ["NS0", "NS1"], 64)
-    ts("e10", T.E1[:], T.EI[:], 1.0, None, ALU.add, None, ["EI"], ["E10", "E11"], 64)
+    cp("nu0", T.NU[:], T.NI[:], ["NI"], ["NU0", "NU1"], 64)
+    cp("ns0", T.NS[:], T.NI[:], ["NI"], ["NS"], 64)
+    for t in range(2):
+        s0 = BASE + K * t
+        dma("old%d" % t, "s", [(T.WIN[:, 2 * K * t + K * h + H:2 * K * t + K * h + K], T.A[:, s0 + H * h:s0 + H * h + H]) for h in range(2)],
+            AK[s0 // H:s0 // H + 2], ["OLD_%d0" % t, "OLD_%d1" % t], 256 * K)
 
-    def gop(name, fn, r, w, n):
-        add(name, "g", lambda: [fn()], r, w, 0.17 + 2 * n * CYC)
     gop("iki", lambda: g.iota(T.KI[:, 0:1], [[0, 1]], 0, 1), [], ["KI0"], 1)
-    gop("ixm", lambda: g.iota(T.XMI[:], [[1, 176]], 97, 0), [], ["XMI"], 176)
-    gop("iiw", lambda: g.iota(T.IWR[:], [[0, 2], [16, 32]], 0, 1, allow_small_or_imprecise_dtypes=True), [], ["IWR"], 64)
-    gop("ione", lambda: g.iota(T.ONES[:], [[0, 576]], 1, 0, allow_small_or_imprecise_dtypes=True), [], ["ONES"], 576)
+    gop("ixx", small(g.iota, T.XX[:], [[0, 2], [1, 128]], 0, 0), [], ["XX"], 256)
+    gop("ixb", small(g.iota, T.XB[:], [[0, 2], [16, 8], [0, 16]], 0, 0), [], ["XB"], 256)
+    gop("iiw", small(g.iota, T.IWR[:], [[0, 2], [16, 32]], H, 1), [], ["IWR"], 64)
+    gop("ick", small(g.iota, col(CK), [[0, 1]], 0, 1), [], ["ck"], 1)
+    gop("isg", small(g.iota, T.SG[:], [[0, 8], [-4096, 16]], 8192, 0), [], ["SG"], 128)
+    gop("sel", lambda: g.affine_select(T.SEL[:], T.ONES[0:8, 0:128], [[-1, 8], [0, 16]], ALU.is_equal, 0.0, 0, 1), ["ONES"], ["SEL"], 128)
+    gop("idw", lambda: g.affine_select(T.IDW[:], T.ONES[:, 0:132], [[-1, 132]], ALU.is_equal, 0.0, 3, 1), ["ONES"], ["IDW"], 132)
     for q in range(4):
         gop("ma%d" % q, lambda q=q: g.affine_select(T.MA[:, 576 * q:576 * q + 576], T.ONES[:], [[-1, 4], [-16, 9], [1000, 16]],
                                                     ALU.is_equal, 0.0, -1000 - 4 * q, 1), ["ONES"], ["MA%d" % q], 576)
-    gop("ick", lambda: g.iota(col(CK), [[0, 1]], 0, 1, allow_small_or_imprecise_dtypes=True), [], ["ck"], 1)
-    gop("ick16", lambda: g.iota(col(CK16), [[0, 1]], 0, 16, allow_small_or_imprecise_dtypes=True), [], ["ck16"], 1)
-    gop("idw", lambda: g.affine_select(T.IDW[:], T.ONES[:, 0:132], [[-1, 132]], ALU.is_equal, 0.0, 3, 1), ["ONES"], ["IDW"], 132)
     ts("kg", T.KI[:, 4:5], T.KI[:, 0:1], 112, None, ALU.bitwise_and, None, ["KI0"], ["KI1"], 1)
     ts("kr", T.KI[:, 5:6], T.KI[:, 0:1], 15, None, ALU.bitwise_and, None, ["KI0"], ["KI2"], 1)
     cp("cr", T.C[:, CG16:CG16 + 2], T.KI[:, 4:6], ["KI1", "KI2"], ["cr", "cg"], 1)
+    for nm, j, b, s in (("cbu", CBU, 0.0, -2.0), ("cb1", CB1, -1.0, -2.0), ("cb961", CB961, -961.0, -2.0),
+                        ("ckt", CKT, 20.0, 1.0), ("crh", CRH, 0.0, 0.5)):
+        act(nm, col(j), col(CR), ACT.Identity, b, s, ["cr"], [nm], 1)
     ts("cm14", col(CM14), col(CR), 13.5, None, ALU.is_ge, None, ["cr"], ["cm14"], 1)
-    ts("cb1", col(CB1), col(CR), -2.0, -1.0, ALU.mult, ALU.add, ["cr"], ["cb1"], 1)
-    ts("cb961", col(CB961), col(CR), -2.0, -961.0, ALU.mult, ALU.add, ["cr"], ["cb961"], 1)
-    ts("cbu", col(CBU), col(CR), -2.0, None, ALU.mult, None, ["cr"], ["cbu"], 1)
-    ts("xm", T.XM[:], T.XMI[:], 127, None, ALU.bitwise_and, None, ["XMI"], ["XM"], 176)
-    ts("xb", T.XB[:], T.XMI[:, 15:175], 112, None, ALU.bitwise_and, None, ["XMI"], ["XB"], 160)
-    ts("sel", T.SEL[:], T.XB[0:8, 16:144], T.C[0:8, CK16:CK16 + 1], None, ALU.is_equal, None, ["XB", "ck16"], ["SEL"], 128)
-    ts("y", T.Y[:], T.XB[:, 0:144], col(CG16), None, ALU.is_equal, None, ["XB", "cg"], ["Y"], 144)
-    ts("yn", T.YN[:], T.XB[:, 0:144], col(CG16), -1.0, ALU.is_equal, ALU.mult, ["XB", "cg"], ["YN"], 144)
     ts("cw1", col(CW1), col(CR), 2.0, -2.0, ALU.is_equal, ALU.mult, ["cr"], ["cw1"], 1)
     ts("cw", col(CW), col(CR), 4.5, col(CW1), ALU.is_lt, ALU.add, ["cr", "cw1"], ["cw"], 1)
     ts("cq1", col(CQ1), col(CR), -3.0, col(CR), ALU.add, ALU.mult, ["cr"], ["cq1"], 1)
     ts("cq2", col(CQ2), col(CQ1), 0.0, 16.0, ALU.not_equal, ALU.mult, ["cq1"], ["cq2"], 1)
     ts("cq3", col(CQ3), col(CR), -2.0, 0.0, ALU.add, ALU.min, ["cr"], ["cq3"], 1)
     ts("cbp", col(CBP), col(CQ3), 8192.0, col(CQ2), ALU.mult, ALU.add, ["cq3", "cq2"], ["cbp"], 1)
-    ts("ep", T.EP[:, 0:143], T.XM[:, 16:159], col(CG16), col(CW), ALU.is_equal, ALU.mult, ["XM", "cg", "cw"], ["EP"], 143)
-    gop("isg", lambda: g.iota(T.SG[:], [[0, 8], [-4096, 16]], 8192, 0, allow_small_or_imprecise_dtypes=True), [], ["SG"], 128)
-    ts("em", T.EM[:, 0:143], T.XM[:, 0:143], col(CG16), col(CM14), ALU.is_equal, ALU.mult, ["XM", "cg", "cm14"], ["EM"], 143)
-    ts("ev", T.EV[:, 0:143], T.XM[:, 32:175], col(CG16), None, ALU.is_equal, None, ["XM", "cg"], ["EV"], 143)
-    ts("ckt", col(CKT), col(CR), 16.0, None, ALU.add, None, ["cr"], ["ckt"], 1)
-    ts("ek", T.EK[:, 0:143], T.XM[:, 32:175], col(CG16), col(CKT), ALU.is_equal, ALU.mult, ["XM", "cg", "ckt"], ["EK"], 143)
-    ts("sh", T.SH[:], T.XM[:, 15:143], col(CK), None, ALU.is_equal, None, ["XM", "ck"], ["SH"], 128)
-    ts("wz2", T.WZ2[:], T.XB[:, 32:160], col(CG16), 2.0, ALU.is_equal, ALU.mult, ["XB", "cg"], ["WZ2"], 128)
+    ts("y", T.Y[:], T.XB[:], col(CG16), None, ALU.is_equal, None, ["XB", "cg"], ["Y"], 256, 0.5)
+    act("yn", T.YN[:], T.Y[:], ACT.Copy, 0.0, -1.0, ["Y"], ["YN"], 256)
+    act("wz2", T.WZ2[:], T.Y[:, 16:144], ACT.Copy, 0.0, 2.0, ["Y"], ["WZ2"], 128)
+    own, nxt, prv = T.XX[:, 113:256], T.XX[:, 97:240], T.XX[:, 1:144]
+    for nm, src, wt, wk in (("EP", own, col(CW), "cw"), ("EM", nxt, col(CM14), "cm14"), ("EV", prv, 2047.0, "cg"),
+                            ("EF", prv, -float(H), "cg"), ("EK", prv, col(CKT), "ckt"), ("EO", own, col(CRH), "crh")):
+        ts(nm.lower(), T[nm][:, 0:143], src, col(CG16), wt, ALU.is_equal, ALU.mult, ["XX", "cg", wk], [nm], 143, 0.5)
+    ts("sh", T.SH[:], T.XX[:, 112:240], col(CK), None, ALU.is_equal, None, ["XX", "ck"], ["SH"], 128, 0.5)
     gop("wz1", lambda: g.affine_select(T.WZ1[:], T.WZ2[:], [[1, 128]], ALU.not_equal, -62.0, 16, -1), ["WZ2"], ["WZ1"], 128)
     gop("wz", lambda: g.affine_select(T.WZ[:], T.WZ1[:], [[1, 128]], ALU.not_equal, -62.0, -112, -1), ["WZ1"], ["WZ"], 128)
     tt("wp", T.WP[:], T.SG[:], T.WZ2[:], ALU.mult, ["SG", "WZ2"], ["WP"], 128, 2)
-    for t in range(2):
-        ts("iw%d" % t, T.XW[:, 128 * t + 64:128 * t + 128], T.IWR[:], col(CG16), float(1 - BASE - K * t), ALU.subtract, ALU.add,
-           ["IWR", "cg"], ["IW%d" % t], 64)
+    ts("iw", T.IW[:], T.IWR[:], col(CG16), None, ALU.subtract, None, ["IWR", "cg"], ["IW"], 32)
 
     for h in range(2):
-        mm("pu%d" % h, [[(T["S%d" % h][:], T.SEL[:], T.U8[:, wide(h)])]], ["SEL", "U8"], ["S%d" % h], H)
+        mm("pu%d" % h, [(T["S%d" % h][:], T.SEL[:], T.U8[:, wide(h)])], ["SEL", "U8"], ["S%d" % h], H)
         act("z0i%d" % h, T.Z0[:, wide(h)], T["S%d" % h][:], ACT.Abs, col(CBU), 2.0, ["cbu"], ["S%d" % h, "Z0%d" % h], H)
 
-    def plus(kind, name, out, in_, c, r, w):
-        if OPT[kind] == "v":
-            ts(name, out, in_, c, None, ALU.add, None, r, w, 64)
-        else:
-            act(name, out, in_, ACT.Identity, c, 1.0, r, w, 64)
-
-    def lookup(name, parts, banks, weights, wk, src, sk, dst, dk, more=None):
+    def lookup(name, parts, banks, c0, weights, wk, src, sk, dst, dk, more=None):
         for j in range(parts):
             hs = [j] if parts == 2 else [0, 1]
             n, nm, bank = H * len(hs), "%s%d" % (name, j), banks[j]
             c = slice(32 * hs[0], 32 * hs[0] + 32 * len(hs))
-            extract("x" + nm, bank, weights, src, H * hs[0], n, [wk] + [sk + str(h) for h in hs])
-            cp("u" + nm, dst[:, c], T[bank][:, 0:n // 16], [], [bank] + [dk + str(h) for h in hs], 64)
+            got, gk = T[bank][:, c0 + c.start:c0 + c.stop], cells(bank, c0 + c.start, n // 16)
+            extract("x" + nm, bank, weights, src, H * hs[0], n, [wk] + [sk + str(h) for h in hs], c0 + c.start)
+            cp("u" + nm, dst[:, c], got, gk, [dk + str(h) for h in hs], 64)
             if more is not None:
-                plus("sn", "s" + nm, T.UPS[:, c], T[bank][:, 0:n // 16], more, [], [bank] + ["UPS%d" % h for h in hs])
+                act("s" + nm, T.UPS[:, c], got, ACT.Identity, more, 1.0, gk, ["UPS%d" % h for h in hs], 64)
 
-    same, up1, nsame, nup1 = T.Y[:, 16:144], T.Y[:, 0:128], T.YN[:, 16:144], T.YN[:, 0:128]
+    def parts(kind, t, h):
+        return [[h]] if OPT[kind][t] == "2" else [[0, 1]] if h == 1 else []
+
+    same, up1, nsame, nup1 = T.Y[:, 0:128], T.Y[:, 112:240], T.YN[:, 0:128], T.YN[:, 112:240]
     for t in range(RO):
         S0 = BASE + K * (t % 2)
         last = t == RO - 1
         n_ = lambda s, h=None, t=t: "%s_%d" % (s, t) if h is None else "%s_%d%d" % (s, t, h)
+        eng = lambda s, h, t=t: OPT[s][2 * t + h]
         wino = 2 * K * t
         for h in range(2):
-            er = T.ER[:, wr(h, 64 * t)]
-            erk = "ER%d%d" % (t, h)
-            pick("mg", h, n_("mg", h), T.MG[:, wide(h)], T.PT[:, 0:E].indirect(er), ["PTs", erk], ["MG%d" % h])
-        lookup(n_("m"), OPT["xm"], ("X1", "X1"), T.EM, "EM", T.MG, "MG", T.MU, "MU")
+            er, erk = T.ER[:, wr(h, 64 * t)], "ER%d%d" % (t, h)
+            pick(eng("mg", h), n_("mg", h), T.MG[:, wide(h)], T.PT[:, 0:E].indirect(er), ["PTs", erk], ["MG%d" % h])
+        lookup(n_("m"), int(OPT["xm"][t]), ("X1", "X1"), 0, T.EM, "EM", T.MG, "MG", T.MU, "MU")
         for h in range(2):
-            er = T.ER[:, wr(h, 64 * t)]
-            erk = "ER%d%d" % (t, h)
+            er, erk = T.ER[:, wr(h, 64 * t)], "ER%d%d" % (t, h)
             o = K * t + H * h
-            pick("cg", h, n_("cg", h), T.CS[:, o:o + H], T.A[:].indirect(T.MU[:, wr(h)]), AK + ["MU%d" % h], [n_("CS", h)])
+            pick(eng("cg", h), n_("cg", h), T.CS[:, o:o + H], T.A[:].indirect(T.MU[:, wr(h)]), AK + ["MU%d" % h], [n_("CS", h)])
             send("c%d%d" % (t, h), rank - 1 - t, rank + 1 + t, T.CL[:, o:o + H], T.CS[:, o:o + H], [n_("CS", h)], [n_("CL", h)], 256 * H)
-            ts(n_("ag", h), T.AS[:, o:o + H], T.AC[:].indirect(er), 1.0, None, ALU.add, None, ["AC", erk], [n_("AS", h)], H, GAT)
+            ts(n_("ag", h), T.AS[:, o:o + H], T.AC[:].indirect(er), -1.0, float(E), ALU.mult, ALU.add, ["AC", erk], [n_("AS", h)], H, "gather")
             send("a%d%d" % (t, h), rank - 1 - t, rank + 1 + t, T.AL[:, o:o + H], T.AS[:, o:o + H], [n_("AS", h)], [n_("AL", h)], 256 * H)
         for h in range(2):
-            pick("pg0", h, n_("pg0", h), T.PG[:, wide(h)], T.PT[:].indirect(T.NO[:, wr(h)]), PK + ["NU%d" % h], ["PG%d" % h])
-        lookup(n_("n1"), OPT["x1"], ("X0", "AB1"), T.EP, "EP", T.PG, "PG", T.N1U, "N1U", float(1 - S0))
+            pick(eng("pg0", h), n_("pg0", h), T.PG[:, wide(h)], T.PT[:].indirect(T.NU[:, wr(h)]), PK + ["NU%d" % h], ["PG%d" % h])
+        lookup(n_("n1"), int(OPT["x1"][t]), *OPT["n1"], T.EP, "EP", T.PG, "PG", T.N1U, "N1U", float(-S0))
         for h in range(2):
-            pick("pg1", h, n_("pg1", h), T.PG2[:, wide(h)], T.PT[:].indirect(T.N1U[:, wr(h)]), PK + ["N1U%d" % h], ["PG2%d" % h])
-        lookup(n_("n2"), OPT["x2"], ("AB0", "AB1"), T.EP, "EP", T.PG2, "PG2", T.N2U, "N2U")
+            pick(eng("pg1", h), n_("pg1", h), T.PG2[:, wide(h)], T.PT[:].indirect(T.N1U[:, wr(h)]), PK + ["N1U%d" % h], ["PG2%d" % h])
+        lookup(n_("n2"), int(OPT["x2"][t]), *OPT["n2"], T.EP, "EP", T.PG2, "PG2", T.N2U, "N2U")
         if not last:
-            plus("ph", n_("ph"), T.PH[:], T.NS[:], 0.0, ["NS0", "NS1"], ["PH"])
-            tt(n_("pl"), T.PL[:], T.NS[:], T.PH[:], ALU.subtract, ["NS0", "NS1", "PH"], ["PL"], 64)
+            act(n_("ph"), T.PH[:], T.NS[:], ACT.Copy, 0.0, 1.0, ["NS"], ["PH"], 64)
+            tt(n_("pl"), T.PL[:], T.NS[:], T.PH[:], ALU.subtract, ["NS", "PH"], ["PL"], 64, 2)
             for h in range(2):
                 zb = "ZB%d" % h
                 for j in range(4):
@@ -260,224 +260,201 @@ def build_ops(g, T, topo, core):
                     for a in range(4 * j, 4 * j + 4):
                         grp += [(T[zb][:, a:H:16], T.MA[:, 144 * a + 1:144 * a + 129], T.PH[:, wr(h)]),
                                 (T[zb][:, a:H:16], T.MA[:, 144 * a:144 * a + 128], T.PL[:, wr(h)])]
-                    mm(n_("pp%d" % j, h), [grp], ["IDW", "PT%d%d" % (t, h), "MA%d" % j, "PH", "PL"], [zb], 512 + (H if j == 0 else 0),
+                    mm(n_("pp%d" % j, h), grp, ["IDW", "PT%d%d" % (t, h), "MA%d" % j, "PH", "PL"], [zb], 512 + (H if j == 0 else 0),
                        j == 0, False)
-                wo, ao = wino + K * h + H, S0 + H * h
-                gop(n_("old", h), lambda wo=wo, ao=ao: g.affine_select(T.WIN[:, wo:wo + H], T.A[:, ao:ao + H], [[0, H]], ALU.is_equal, 0.0, 0, 0),
-                    ["A%d" % (ao // AW)], [n_("OLD", h)], H)
+        else:
+            mm("xu", [(T.ZB0[:, 0:64], T.EO[:, 15 - a:143 - a], T.Z0[:, 64 * a:64 * a + 64]) for a in range(16)],
+               ["EO", "Z00", "Z01"], ["ZB0"], 1024)
+            act("uo", T.UO[:], T.ZB0[:, 0:64], ACT.Identity, -40.0, 1.0, [], ["ZB0", "UO"], 64)
         for h in range(2):
-            sbk, zb, ab, xb = "S%d" % h, "ZB%d" % h, "AB%d" % h, "X%d" % h
-            lists = (("NU", T.NO), ("N1U", T.N1U), ("N2U", T.N2U))
+            sbk, zb, ab = "S%d" % h, "ZB%d" % h, "AB%d" % h
+            lists = (("NU", T.NU), ("N1U", T.N1U), ("N2U", T.N2U))
             marks = (("Z0", T.Z0), ("Z1", T.Z1), ("Z2", T.Z2))
             tk, ttv = "TT%d" % h, T.TT[:, wide(h)]
+            by_act = eng("hit", h) == "a"
             for s in range(3):
                 zk, z = marks[s][0] + str(h), marks[s][1][:, wide(h)]
-                tt(n_("g%d" % s, h), ttv, T.A[:].indirect(lists[s][1][:, wr(h)]), z, ALU.max,
-                   AK + [zk, lists[s][0] + str(h)], [tk], H, GAT)
-                pos, neg = (same, nsame) if s < 2 else (up1, nup1)
-                grp = [(T[sbk][:], pos, ttv)]
+                column, ck = T.A[:].indirect(lists[s][1][:, wr(h)]), AK + [lists[s][0] + str(h)]
+                if eng("g%d" % s, h) == "f":
+                    tt(n_("g%d" % s, h), ttv, column, z, ALU.max, ck + [zk], [tk], H, "gather2")
+                else:
+                    gc, gk = T.GC[:, K * s + H * h:K * s + H * h + H], "GC%d%d" % (s, h)
+                    pick(eng("g%d" % s, h), n_("gc%d" % s, h), gc, column, ck, [gk])
+                    mm(n_("pm%d" % s, h), [(T[ab][:], T.IDW[:, 3:131], z)], ["IDW", zk], [ab], H)
+                    tt(n_("g%d" % s, h), ttv, T[ab][:], gc, ALU.max, [gk], [ab, tk], H)
+                pos, neg = (same, nsame) if s < 2 else (nup1, up1) if by_act else (up1, nup1)
+                opens = True
                 if s > 0 or t == 0:
-                    grp = [(T[sbk][:], neg, z)] + grp
-                mm(n_("ps%d" % s, h), [grp], ["Y", "YN", zk, tk], [sbk], H * len(grp))
+                    mm(n_("pn%d" % s, h), [(T[sbk][:], neg, z)], ["Y", "YN", zk], [sbk], H, True, False)
+                    opens = False
+                mm(n_("ps%d" % s, h), [(T[sbk][:], pos, ttv)], ["Y", "YN", tk], [sbk], H, opens, not (s == 2 and by_act))
                 if s < 2:
                     bk, b = ("cb961", CB961) if (s == 0 and t > 0) else ("cb1", CB1)
                     act(n_("z%d" % (s + 1), h), marks[s + 1][1][:, wide(h)], T[sbk][:], ACT.Abs, col(b), 64.0,
                         [bk], [sbk, marks[s + 1][0] + str(h)], H)
             o = K * t + H * h
             hk, hv = "HIT%d" % h, T.HIT[:, wide(h)]
-            tt(n_("hit", h), hv, T[sbk][:], T.CL[:, o:o + H], ALU.is_equal, [n_("CL", h)], [sbk, hk], H)
-            mm(n_("pa", h), [[(T[ab][:], T.SH[:], T.AL[:, o:o + H])]], ["SH", n_("AL", h)], [ab], H)
+            if by_act:
+                mm(n_("pc", h), [(T[sbk][:], T.IDW[:, 3:131], T.CL[:, o:o + H])], ["IDW", n_("CL", h)], [sbk], H, False, True)
+                act(n_("far", h), T.Z1[:, wide(h)], T[sbk][:], ACT.Abs, 0.0, 64.0, [], [sbk, "Z1%d" % h], H)
+                act(n_("hit", h), hv, T.Z1[:, wide(h)], ACT.Relu, 1.0, -1.0, ["Z1%d" % h], [hk], H)
+            else:
+                tt(n_("hit", h), hv, T[sbk][:], T.CL[:, o:o + H], ALU.is_equal, [n_("CL", h)], [sbk, hk], H)
+            mm(n_("pa", h), [(T[ab][:], T.SH[:], T.AL[:, o:o + H])], ["SH", n_("AL", h)], [ab], H)
             tt(n_("val", h), T.VAL[:, wide(h)], T[ab][:], hv, ALU.mult, [hk], [ab, "VAL%d" % h], H)
-            extract(n_("xv", h), "X0", T.EV, T.VAL, H * h, H, ["EV", "VAL%d" % h], 32 * h)
+            for hs in ([] if last else parts("xf", t, h)):
+                c, n = slice(32 * hs[0], 32 * hs[-1] + 32), 32 * len(hs)
+                extract(n_("xf", h), "X1", T.EF, T.HIT, H * hs[0], 16 * n, ["EF", "SH", "IW"] + ["HIT%d" % j for j in hs], 64 + c.start,
+                        [(T.SH[:], T.IW[:, 0:n])])
+                cp(n_("ou", h), T.OU[:, c], T.X1[:, 64 + c.start:64 + c.stop], cells("X1", 64 + c.start, n), ["OU%d" % j for j in hs], n)
+            for hs in parts("xv", t, h):
+                extract(n_("xv", h), "X0", T.EV, T.VAL, H * hs[0], H * len(hs), ["EV"] + ["VAL%d" % j for j in hs], 32 * hs[0])
             if not last:
                 dma("sh%d%d" % (t, h), "s", [(T.WIN[0:112, wino + K * h:wino + K * h + H], T.CL[16:128, o:o + H]),
                                              (T.WIN[112:128, wino + K * h:wino + K * h + H], T.CL[0:16, o:o + H])],
                     [n_("CL", h)], [n_("NEW", h)], 256 * H)
-                mm(n_("pq", h), [[(T[zb][:], T.WP[:], hv)]], ["WP", hk], [zb], H, False, True)
-                mm(n_("pz", h), [[(T[sbk][:], T.IDW[:, 3:131], T.Z0[:, wide(h)]), (T[sbk][:], T.WZ[:], hv)]],
-                   ["IDW", "WZ", "Z0%d" % h, hk], [sbk], 2 * H)
+                mm(n_("pq", h), [(T[zb][:], T.WP[:], hv)], ["WP", hk], [zb], H, False, True)
+                mm(n_("py", h), [(T[sbk][:], T.IDW[:, 3:131], T.Z0[:, wide(h)])], ["IDW", "Z0%d" % h], [sbk], H, True, False)
+                mm(n_("pz", h), [(T[sbk][:], T.WZ[:], hv)], ["WZ", hk], [sbk], H, False, True)
                 act(n_("z0", h), T.Z0[:, wide(h)], T[sbk][:], ACT.Sign, -0.5, 1.0, [], [sbk, "Z0%d" % h], H)
-            for hs in ([[h]] if not last else [[0, 1]] if h == 1 else []):
+            for hs in parts("xv", t, h):
                 c = slice(32 * hs[0], 32 * hs[-1] + 32)
-                X = T.X0[:, c]
                 k_ = lambda s, hs=hs: [s + str(j) for j in hs]
-                ts(n_("nok", h), T.NOK[:, c], X, 0.0, None, ALU.is_equal, None, [], ["X0"] + k_("NOK"), 32)
-                tt(n_("te", h), T.TE[:, c], T.NOK[:, c], T.E1[:, c], ALU.mult, k_("NOK") + k_("E1"), k_("TE"), 32)
-                tt(n_("e1", h), T.E1[:, c], X, T.TE[:, c], ALU.add, k_("TE"), ["X0"] + k_("E1"), 32)
+                old, ok_ = (T.EI, ["EI"]) if t == 0 else (T.EN, k_("EN"))
+                tt(n_("ey", h), T.EY[:, c], T.X0[:, c], old[:, c], ALU.max, ok_ + k_("X0:"), k_("EY"), 32)
+                ts(n_("en", h), T.EN[:, c], T.EY[:, c], E - 1, None, ALU.bitwise_and, None, k_("EY"), k_("EN"), 32)
                 if last:
-                    plus("ef", n_("ef", h), T.EF[:], T.E1[:], -1.0, k_("E1"), k_("EF"))
+                    cp("ew", T.EW[:], T.EN[:], k_("EN"), ["EW"], 64)
                     continue
-                euk = "EU%d%d" % (t + 1, h)
-                ts(n_("eu", h), T.EU[:, wr(h, 64 * t + 64)], T.E1[:, c], -1.0, None, ALU.add, None, k_("E1"), [euk], 32)
-                send("e%d%d" % (t + 1, h), rank + 2 + t, rank - 2 - t, T.ER[:, wr(h, 64 * t + 64)], T.EU[:, wr(h, 64 * t + 64)],
-                     [euk], ["ER%d%d" % (t + 1, h)], 8192)
-        xb, nw = T.XW[:, 128 * (t % 2):128 * (t % 2) + 64], (64 if last else 128)
-        ts(n_("tb"), T.TB[:], T.X0[:, 0:64], 1024.5, -1024.0, ALU.is_gt, ALU.mult, [], ["X0", "TB"], 64)
-        tt(n_("tn2"), xb, T.X0[:, 0:64], T.TB[:], ALU.add, ["TB"], ["X0", "TN2"], 64)
-        tt(n_("tn"), T.TN[:, 0:64], T.NOK[:], T.UPS[:], ALU.mult, ["NOK0", "NOK1", "UPS0", "UPS1"], ["TN"], 64)
-        if not last:
-            ts(n_("to"), T.TN[:, 64:128], T.X0[:, 0:64], 0.0, float(H), ALU.is_equal, ALU.mult, [], ["X0", "TO"], 64)
-        tt(n_("tn3"), T.TD[:, 0:nw], T.XW[:, 128 * (t % 2):128 * (t % 2) + nw], T.TN[:, 0:nw], ALU.add,
-           ["TN2", "TN", "TO", "IW%d" % (t % 2)], ["TD"], nw, 2 if nw > 64 else 1)
-        if not last:
-            ts(n_("nu"), T.NO[:], T.TD[:], float(S0 - 1), None, ALU.add, None, ["TD"], ["NU0", "NU1", "OU0", "OU1"], 128)
-        plus("nl" if last else "ns", n_("ns"), T.NS[:], T.TD[:, 0:64], float(S0 - 1), ["TD"], ["NS0", "NS1"])
-        kb = "S0" if last else "AB0"
-        grp = [(T[kb][:, 0:64], T.EK[:, 15 - a:143 - a], T.HIT[:, 64 * a:64 * a + 64]) for a in range(16)]
-        mm(n_("xk"), [grp], ["EK", "HIT0", "HIT1"], [kb], 1024)
-        tt(n_("u"), T.UJ[:], T[kb][:, 0:64], T.UK[:], ALU.max, ["UK"], [kb, "UJ"], 64)
-        ts(n_("uk"), T.UK[:], T.UJ[:], 15, None, ALU.bitwise_and, None, ["UJ"], ["UK"], 64)
+                euk, ce = "EU%d%d" % (t + 1, h), slice(64 * t + 64 + c.start, 64 * t + 64 + c.stop)
+                cp(n_("eu", h), T.EU[:, ce], T.EN[:, c], k_("EN"), [euk], 32)
+                send("e%d%d" % (t + 1, h), rank + 2 + t, rank - 2 - t, T.ER[:, ce], T.EU[:, ce], [euk], k_("ER%d" % (t + 1)), 8192 * len(hs))
         if last:
-            cp("uf", T.UF[:], T.UK[:], ["UK"], ["UF"], 64)
+            ts(n_("nok"), T.NOK[:], T.X0[:, 0:64], 0.0, None, ALU.is_equal, None, cells("X0", 0, 64), ["NOK"], 64)
+        else:
+            ts(n_("nok"), T.NOK[:], T.X1[:, 64:128], float(H), None, ALU.is_ge, None, cells("X1", 64, 64), ["NOK"], 64)
+        tt(n_("tn"), T.TN[:], T.NOK[:], T.UPS[:], ALU.mult, ["NOK", "UPS0", "UPS1"], ["TN"], 64, 2)
+        cp(n_("xi"), T.XI[:], T.X0[:, 0:64], cells("X0", 0, 64), ["XI"], 64)
+        ts(n_("xl"), T.XL[:], T.XI[:], K - 1, None, ALU.bitwise_and, None, ["XI"], ["XL"], 64)
+        tt(n_("td"), T.TD[:], T.XL[:], T.TN[:], ALU.add, ["XL", "TN"], ["TD"], 64, 2)
         if not last:
+            ts(n_("nu"), T.NU[:], T.TD[:], float(S0), None, ALU.add, None, ["TD"], ["NU0", "NU1"], 64)
+        if t != 1:
+            act(n_("ns"), T.NS[:], T.TD[:], ACT.Identity, float(S0), 1.0, ["TD"], ["NS"], 64)
+        if last:
+            mm("xk", [(T.ZB1[:, 0:64], T.EK[:, 15 - a:143 - a], T.HIT[:, 64 * a:64 * a + 64]) for a in range(16)],
+               ["EK", "HIT0", "HIT1"], ["ZB1"], 1024)
+            tt("uj", T.UJ[:], T.ZB1[:, 0:64], T.UO[:], ALU.max, ["UO"], ["ZB1", "UJ"], 64)
+            act("uf", T.UF[:], T.UJ[:], ACT.Abs, -20.0, 1.0, ["UJ"], ["UF"], 64)
+        else:
             for h in range(2):
-                zb = "ZB%d" % h
-                a_out, a_in = T.A[:, S0 + H * h:S0 + H * h + H], T.WIN[:, wino + K * h:wino + K * h + K].indirect(T.NO[:, wr(h, 64)])
-                rk, wk = [n_("OLD", h), n_("NEW", h), "OU%d" % h], ["A%d" % ((S0 + H * h) // AW)]
-                pick("ins", h, n_("ins", h), a_out, a_in, rk, wk)
-                act(n_("pe", h), T.PT[:, S0 + H * h:S0 + H * h + H], T[zb][:], ACT.Relu, col(CBP), 1.0, ["cbp"], [zb, "PT%d%d" % (t, h)], H)
-    dma("oe", "s", [(T.ye[:], T.EF[:])], ["EF0", "EF1"], [], 32768)
-    dma("on", "a", [(T.yn[:], T.NS[:])], ["NS0", "NS1"], [], 32768)
-    dma("ou", "s", [(T.yu[:], T.UF[:])], ["UF"], [], 32768)
+                zb, ao = "ZB%d" % h, S0 + H * h
+                pick(eng("ins", h), n_("ins", h), T.A[:, ao:ao + H], T.WIN[:, wino + K * h:wino + K * h + K].indirect(T.OU[:, wr(h)]),
+                     [n_("OLD", h), n_("NEW", h), "OU%d" % h], ["A%d" % (ao // H)])
+                act(n_("pe", h), T.PT[:, ao:ao + H], T[zb][:], ACT.Relu, col(CBP), 1.0, ["cbp"], [zb, "PT%d%d" % (t, h)], H)
+    dma("ou", "a", [(T.yu[:], T.UF[:])], ["UF"], [], 32768)
+    dma("oe", "s", [(T.ye[:], T.EW[:])], ["EW"], [], 32768)
+    dma("on", "a", [(T.yn[:], T.NS[:])], ["NS"], [], 32768)
     return ops
 
 
 def deps_of(ops):
+    def pieces(keys):
+        return [p for k in keys for p in (["%s:%d" % (k, c) for c in range(6)] if k in BANKS else [k])]
+
     lw, rd, out = {}, {}, []
     for i, o in enumerate(ops):
-        d = set()
-        for k in o["r"]:
-            if k in lw:
-                d.add(lw[k])
         look = [k for k in o["w"] if k in BANKS and o["q"] != "p"]
-        for k in o["w"]:
-            if k in lw:
-                d.add(lw[k])
-            d.update(j for j in rd.get(k, []) if k not in look or ops[j]["q"] != o["q"])
+        reads, writes = pieces(o["r"] + look), pieces([k for k in o["w"] if k not in look])
+        d = set(lw[k] for k in reads + writes if k in lw)
+        for k in writes:
+            d.update(rd.get(k, []))
         d.discard(i)
         out.append(sorted(d))
-        for k in o["r"] + look:
+        for k in reads:
             rd.setdefault(k, []).append(i)
-        for k in o["w"]:
-            if k not in look:
-                lw[k] = i
-                rd[k] = []
+        for k in writes:
+            lw[k] = i
+            rd[k] = []
     return out
 
 
-def play(ops, deps, prio, gat=1.0, pe=1.0, net=1.0, order=None):
-    n = len(ops)
-    name = {o["name"]: i for i, o in enumerate(ops)}
-    succ = [[] for _ in ops]
-    left = [0] * n
-    for i in range(n):
-        pre = list(deps[i]) + ([name[ops[i]["after"]]] if "after" in ops[i] else [])
-        left[i] = len(pre)
-        for d in pre:
-            succ[d].append(i)
-    end, start, rdy = [0.0] * n, [0.0] * n, [0.0] * n
-    free = {"v": 0.0, "a": 0.0, "p": 0.0, "g": 0.0, "s": 0.0, "D": 0.0, "R": 0.0}
-    ready = [i for i in range(n) if left[i] == 0]
-    seq = []
-    pos = 0
-    first = [True]
-    while ready:
-        if order is not None:
-            i = order[pos]
-            pos += 1
-        else:
-            best = None
-            for j in ready:
-                q = ops[j]["q"]
-                st = rdy[j] if q is None else max(rdy[j], free[q])
-                key = (-1e9 if q is None else st - prio[j], j)
-                if best is None or key < best[0]:
-                    best = (key, j)
-            i = best[1]
-        ready.remove(i)
-        o = ops[i]
-        q = o["q"]
-        st = rdy[i] if q is None else max(rdy[i], free[q])
-        start[i] = st
-        dur = o["dur"]
-        if o["kind"] == "c":
-            if q == "p":
-                dur *= pe
-            elif dur > 0.8 and dur < 1.0 and q != "g":
-                dur *= gat
-            free[q] = end[i] = st + dur
-        elif o["kind"] == "d":
-            free[q] = st + dur
-            b = max(st + dur + DFIX * 0.7, free["D"])
-            free["D"] = b + o["x"] / DRATE * net
-            end[i] = free["D"] + DFIX * 0.3
-        elif o["kind"] == "s":
-            free[q] = st + dur + (1.0 if first[0] else 0.0)
-            first[0] = False
-            b = max(free[q] + RFIX * 0.6 * net, free["D"], free["R"])
-            free["R"] = b + o["x"][0] / RRATE * net
-            end[i] = free["R"] + RFIX * 0.4 * net
-        else:
-            end[i] = st
-        seq.append(i)
-        for j in succ[i]:
-            if ops[j].get("after") == o["name"] or (o["kind"] == "s" and ops[j]["kind"] != "r"):
-                t = free[q]
-            elif o["kind"] == "s" or (q == "p" and ops[j]["q"] == "p"):
-                t = end[i] if q != "p" else 0.0
-            else:
-                t = end[i] + SEM
-            rdy[j] = max(rdy[j], t)
-            left[j] -= 1
-            if left[j] == 0:
-                ready.append(j)
-    return seq, start, end
+def banks_of(o):
+    return sorted(set(k.split(":")[0] for k in o["r"] + o["w"]) & set(BANKS))
 
 
-MODELS = ((1.0, 1.0, 1.0), (0.7, 0.8, 0.8), (1.3, 1.0, 1.0), (1.0, 1.5, 1.3), (0.7, 1.0, 1.4))
-DIGITS = "0123456789abcdefghijklmnopqrstuvwxyzABCDEFGHIJKLMNOPQRSTUVWXYZ"
-ORDER = "0205010006070v0t0s0B0C0w0A0c0x0W0y0b0E0D0L0F030P0R0f0q0g0J0I0G0K0O0N0p0M0Q110Y0T0X120S0804090j0h0a0i1F0k0d181a0l1G0Z0V0n0e0r1v0o0m190H1R101b1c1u1d1M1N1e1w1f1S1g2d151h1x2e1O1H1I1i1l0u1j0z1T1U2f1o1z1J1V1K1B1W1A2g1r1C162h2i1y1m1p131s141X1n1D1Y1E172j201k1t1q2k1Z0U252122242m1P2l2728292a2n2q2o2p232r2G2t2z2u2B2A2C2v2D2K2M262s2b1L1Q2c2F2N3g2w2E2W2L3h2P2Q3i2J3s2x353j363t3n372T3u2y2O3O3P3k2R383a3Q2H3v3w322S3x2Z2X2U33302Y3R2V3b34313c3d3S3B3y3T393z3A3e3l3o3p3f3C3U3D3q3I3J3K2I3V3X3F3G3L3W3Y3M3m3r3E403N3Z414l3H4n444d454a464b4c474e4f4x4m4o424h4q4r4H48494k434G4u4I4R4J534D4p4S4s4t4T4L4y4z54554A4U4i564V4N4O4W574M584K4g4v4E4F4P4X4Y504j4Q595c5a4w4B4C4Z515b5d525o5e5p5q5r5j5f5k5l5g5m5h5n5u5i5t5s"
-PLAN = {}
-TRIES = 120
+def in_turns(ops, deps, seq):
+    out, last = [list(d) for d in deps], {}
+    for i in seq:
+        for b in banks_of(ops[i]):
+            seen = last.setdefault(b, {})
+            out[i] += [j for q, j in seen.items() if q != ops[i]["q"]]
+            seen[ops[i]["q"]] = i
+    return out
+
+
+ORDER = """
+lu le li0 lp fill0 ixb ixx iki fill2 fill3 fill1 ones kr kg ns0 cr ub y cm14 cw1 dhi dlo nu0 li1 li3 lu8 li2 li5 se00
+li4 sel ick ma0 idw lpt lac pu1 pu0 cv0 cbu ph_0 ckt yn cv1 cb1 z0i1 wz2 z0i0 cv2 pg0_01 pg0_00 cv3 pl_0 cw cq1 em cv5
+ep er0 cv4 cq2 ef sh mg_00 pn0_01 pp0_00 pn0_00 xm_00 pp0_01 xn1_01 xn1_00 g0_01 um_00 cq3 g0_00 un1_01 un1_00 cbp ag_00
+cg_00 mg_01 iiw ma1 ma2 isg ma3 wz1 sc00 sa00 old0 ps0_00 pp1_01 pp2_01 xm_01 pp1_00 ps0_01 z1_00 pg1_01 g1_00 ag_01
+z1_01 pg1_00 xn2_01 pn1_00 pn1_01 ps1_00 um_01 g1_01 xn2_00 z2_00 un2_00 ek g2_00 wp ev pp2_00 pp3_01 pn2_00 ps1_01
+pp3_00 cg_01 sn1_00 z2_01 sn1_01 sa01 sc01 wz sh00 ps2_00 pn2_01 pa_00 hit_00 un2_01 iw g2_01 pq_00 xf_00 pa_01 py_00
+sh01 ps2_01 pz_00 ou_00 val_00 hit_01 xv_00 ey_00 val_01 en_00 pq_01 xf_01 eu_00 ou_01 nok_0 xv_01 pe_00 cb961 ins_00
+z0_00 crh pe_01 ins_01 se10 py_01 tn_0 xi_0 ey_01 xl_0 en_01 td_0 eu_01 nu_0 pg0_11 g0_10 pz_01 ns_0 z0_01 pg0_10 mg_10
+ph_1 xn1_10 xm_10 ps0_10 ag_10 pl_1 un1_10 um_10 g0_11 se11 mg_11 cg_10 z1_10 pp0_10 xm_11 pp0_11 ps0_11 pp1_11 pg1_10
+ag_11 um_11 g1_10 z1_11 cg_11 xn2_10 pn1_10 pn1_11 ps1_10 un2_10 g1_11 sa10 old1 sc10 sa11 sc11 sh10 pp1_10 pa_10 z2_10
+pp2_10 pn2_10 ps1_11 pp2_11 g2_10 pg1_11 z2_11 ps2_10 xn2_11 hit_10 un2_11 val_10 g2_11 pp3_11 py_10 pn2_11 xv_10 sn1_10
+pa_11 pz_10 ey_10 z0_10 ps2_11 en_10 eu_10 xf_10 hit_11 se20 sh11 ou_10 val_11 xf_11 ins_10 xv_11 nok_1 eo tn_1 ou_11
+ey_11 xi_1 en_11 xl_1 eu_11 td_1 ins_11 ag_20 nu_1 pq_11 pp3_10 py_11 pz_11 pq_10 pe_11 mg_20 pe_10 z0_11 se21 xm_20
+um_20 sa20 g0_20 g0_21 pg0_20 cg_20 mg_21 ps0_20 xu xm_21 sc20 pg0_21 z1_20 um_21 xn1_20 ps0_21 pn1_20 cg_21 ag_21
+un1_20 g1_20 sc21 sa21 z1_21 pg1_20 g1_21 ps1_20 xn2_20 pa_20 pn1_21 z2_20 pg1_21 un2_20 g2_20 ps1_21 xn2_21 un2_21
+sn1_20 z2_21 uo g2_21 pn2_20 pn2_21 ps2_20 ps2_21 hit_20 pa_21 hit_21 val_20 xk val_21 xv_21 uj nok_2 xi_2 tn_2 ey_21
+xl_2 en_21 td_2 ew uf ou oe ns_2 on
+"""
 
 
 def plan(ops, deps):
-    if ORDER:
-        seq = [DIGITS.index(ORDER[i]) * 62 + DIGITS.index(ORDER[i + 1]) for i in range(0, len(ORDER), 2)]
-        assert sorted(seq) == list(range(len(ops)))
-        place = {j: p for p, j in enumerate(seq)}
-        assert all(place[d] < place[i] for i in seq for d in deps[i])
-        return seq
-    if "seq" in PLAN:
-        return PLAN["seq"]
-    n = len(ops)
-    tail = [0.0] * n
-    for i in range(n - 1, -1, -1):
-        o = ops[i]
-        tail[i] += o["dur"] + SEM + (DFIX + o["x"] / DRATE if o["kind"] == "d" else RFIX + o["x"][0] / RRATE if o["kind"] == "s" else 0.0)
-        for d in deps[i]:
-            tail[d] = max(tail[d], tail[i])
-    rng = np.random.RandomState(1)
-    best = None
-    for k in range(TRIES):
-        wgt = (0.05, 0.1, 0.2, 0.4)[k % 4]
-        noise = rng.rand(n) * (0.0 if k < 4 else 0.3)
-        prio = [wgt * tail[i] + wgt * 4 * float(noise[i]) for i in range(n)]
-        seq, _s, _e = play(ops, deps, prio)
-        cost = sum(max(play(ops, deps, None, a, b, c, seq)[2]) for a, b, c in MODELS)
-        if best is None or cost < best[0]:
-            best = (cost, seq)
-    PLAN["seq"] = best[1]
-    PLAN["cost"] = best[0] / len(MODELS)
-    return best[1]
+    index = {o["name"]: i for i, o in enumerate(ops)}
+    seq = []
+    for s in ORDER.split():
+        seq.append(index[s])
+        if ops[index[s]]["kind"] == "s":
+            seq.append(index["r" + s[1:]])
+    assert sorted(seq) == list(range(len(ops)))
+    place = {j: p for p, j in enumerate(seq)}
+    assert all(place[d] < place[i] for i in seq for d in deps[i])
+    return seq
+
+
+def helper_of(core, T, topo):
+    return [c for c in topo.cores_of(core) if T.rank_of(c) is None and topo.die(c) == topo.die(core)
+            and topo.addr(c)[2] != topo.addr(core)[2]][0]
+
+
+def helper_program(g, core, owner, T, topo):
+    sent = 0
+    for name in RELAYED:
+        t, h = int(name[1]), int(name[2])
+        dst = T.cores[(T.rank_of(owner) - 1 - t) % N]
+        rid, pid, _se = topo.addr(dst)
+        piece = T.AL[:, K * t + H * h:K * t + H * h + H]
+        g.wait_ge(T.sem["h" + name], len(topo.engines(owner, core)) - len(topo.engines(owner, dst)))
+        g.remote_dma(piece, piece, T.sem["r" + name], T.sem.loc, pid, rid, topo.mask(core, dst))
+        sent += len(topo.engines(core, dst))
+    g.wait_ge(T.sem.loc, sent)
 
 
 def rank_program(g, core, T, topo):
     if T.rank_of(core) is None:
+        for owner in T.cores:
+            if helper_of(owner, T, topo) == core:
+                helper_program(g, core, owner, T, topo)
         return
     ops = build_ops(g, T, topo, core)
     deps = deps_of(ops)
     seq = plan(ops, deps)
+    deps = in_turns(ops, deps, seq)
     queue = {"v": g.vector, "a": g.scalar, "p": g.tensor, "g": g, "s": g.sync}
     csem = {"v": "cv", "a": "ca", "p": "cp", "g": "cg"}
     known = {q: {} for q in queue}

from concourse.mybir import AluOpType, ActivationFunctionType

N, BASE, K, E, W, RO = 8, 4096, 1024, 2048, 6144, 3
H = 512
NCH = 6
ALU = AluOpType
ACT = ActivationFunctionType


def sb(n, d, p=128):
    return ("sbuf", [p, n], d)


SCRATCH = {
    "A": sb(W, "bfloat16"), "PT": sb(W, "bfloat16"), "AC": sb(E, "int32"),
    "DEN": sb(512, "int32"), "DHI": sb(512, "bfloat16"), "DLO": sb(512, "bfloat16"),
    "EI": sb(64, "int32"), "NI": sb(64, "int32"), "UK": sb(64, "int32"), "ERI": sb(64, "int32"),
    "UB": sb(64, "bfloat16"), "IDW": sb(132, "bfloat16"), "U8": sb(K, "bfloat16", 8),
    "XX": sb(256, "bfloat16"), "XB": sb(256, "bfloat16"), "KI": sb(8, "int32"), "C": sb(24, "float32"),
    "SG": sb(128, "bfloat16"), "WP": sb(128, "bfloat16"), "Y": sb(256, "bfloat16"), "YN": sb(256, "bfloat16"),
    "SH": sb(128, "float16"), "WZ1": sb(128, "bfloat16"), "WZ2": sb(128, "bfloat16"), "WZ": sb(128, "bfloat16"),
    "SEL": sb(128, "bfloat16", 8), "EP": sb(144, "bfloat16"), "EM": sb(144, "bfloat16"), "EV": sb(144, "float16"),
    "EK": sb(144, "bfloat16"), "EO": sb(144, "bfloat16"), "EF": sb(144, "bfloat16"),
    "ONES": sb(576, "bfloat16"), "MA": sb(16 * 144, "bfloat16"), "IWR": sb(64, "float32"), "IW": sb(64, "float16"),
    "EU": sb(3 * 64, "uint16"), "ER": sb(3 * 64, "uint16"), "NU": sb(64, "uint16"), "OU": sb(64, "uint16"),
    "N1U": sb(64, "uint16"), "N2U": sb(64, "uint16"), "MU": sb(64, "uint16"),
    "EY": sb(64, "int32"), "EN": sb(64, "int32"), "XI": sb(64, "int32"), "XL": sb(64, "int32"),
    "NS": sb(64, "float32"), "UPS": sb(64, "float32"), "UO": sb(64, "float32"), "UJ": sb(64, "float32"),
    "UF": sb(64, "float32"), "EW": sb(64, "float32"), "NOK": sb(64, "float32"), "TN": sb(64, "float32"),
    "TD": sb(64, "float32"), "PH": sb(64, "bfloat16"), "PL": sb(64, "bfloat16"),
    "PG": sb(K, "bfloat16"), "PG2": sb(K, "bfloat16"), "MG": sb(K, "bfloat16"),
    "Z0": sb(K, "bfloat16"), "Z1": sb(K, "bfloat16"), "Z2": sb(K, "bfloat16"), "TT": sb(K, "bfloat16"),
    "HIT": sb(K, "bfloat16"), "VAL": sb(K, "float16"),
    "CS": sb(3 * K, "bfloat16"), "CL": sb(3 * K, "bfloat16"), "AS": sb(3 * K, "float16"), "AL": sb(3 * K, "float16"),
    "WIN": sb(4 * K, "bfloat16"), "GC": sb(3 * K, "bfloat16"),
    "S0": ("psum", [128, 512], "float32"), "S1": ("psum", [128, 512], "float32"),
    "ZB0": ("psum", [128, 512], "float32"), "ZB1": ("psum", [128, 512], "float32"),
    "AB0": ("psum", [128, 512], "float32"), "AB1": ("psum", [128, 512], "float32"),
    "X0": ("psum", [128, 512], "float32"), "X1": ("psum", [128, 512], "float32"),
}
BANKS = [k for k, v in SCRATCH.items() if v[0] == "psum"]
DMAS = (["le", "lp", "lu", "lu8", "lpt", "lac", "oe", "on", "ou", "old0", "old1"] + ["li%d" % i for i in range(NCH)]
        + ["sh%d%d" % (t, h) for t in range(2) for h in range(2)])
ARR = (["re00"] + ["re%d%d" % (t, h) for t in (1, 2) for h in range(2)]
       + ["r%s%d%d" % (x, t, h) for x in "ca" for t in range(3) for h in range(2)])
RELAYED = []
SEMAPHORES = ["cv", "ca", "cp", "cg", "loc"] + DMAS + ARR + ["h" + n for n in RELAYED]

CK, CG16, CR, CM14, CB1, CB961, CBU, CKT, CRH, CW1, CW, CQ1, CQ2, CQ3, CBP = range(15)
OPT = {"mg": "vaaaaa", "cg": "aaaaaa", "pg0": "aaavva", "pg1": "aaaaaa", "ins": "aaav", "hit": "vvvvvv", "cv": "aaavvv",
       "g0": "ffffff", "g1": "ffffff", "g2": "ffffff", "n1": (("X0", "X0"), 64), "n2": (("X1", "X1"), 128),
       "x1": "211", "x2": "222", "xm": "222", "xf": "22", "xv": "221", "lq": "ssssss"}


def build_ops(g, T, topo, core):
    ops = []
    rank = T.rank_of(core)
    V, S, P = g.vector, g.scalar, g.tensor

    def add(name, q, fn, r, w, size, kind="c", extra=None):
        ops.append({"name": name, "q": q, "fn": fn, "r": r, "w": w, "size": size, "kind": kind, "x": extra})

    def ts(name, out, in0, s1, s2, op0, op1, r, w, n, f=1.0):
        if op1 is None:
            add(name, "v", lambda: [V.tensor_scalar(out, in0, s1, None, op0)], r, w, (n, f))
        else:
            add(name, "v", lambda: [V.tensor_scalar(out, in0, s1, s2, op0, op1)], r, w, (n, f))

    def tt(name, out, in0, in1, op, r, w, n, f=1.0):
        add(name, "v", lambda: [V.tensor_tensor(out, in0, in1, op)], r, w, (n, f))

    def cp(name, out, in_, r, w, n, f=1.0):
        add(name, "v", lambda: [V.tensor_copy(out, in_)], r, w, (n, f))

    def act(name, out, in_, func, bias, scale, r, w, n, f=1.0):
        add(name, "a", lambda: [S.activation(out, in_, func, bias=bias, scale=scale)], r, w, (n, f))

    def gop(name, fn, r, w, n):
        add(name, "g", lambda: [fn()], r, w, (n, 2.0))

    def pick(eng, name, out, in_, r, w):
        if eng == "v":
            cp(name, out, in_, r, w, H, "gather")
        else:
            act(name, out, in_, ACT.Copy, 0.0, 1.0, r, w, H, "gather")

    def mm(name, grp, r, w, cyc, opens=True, closes=True):
        def fn():
            for i, (o, l, x) in enumerate(grp):
                ins = P.matmul(o, l, x, opens and i == 0, closes and i == len(grp) - 1)
            return [ins]
        add(name, "p", fn, r, w, (cyc, 1.0))

    def dma(name, q, pairs, r, w, nbytes):
        eng = g.sync if q == "s" else g.scalar
        add(name, q, lambda: [eng.dma_start(o, i) for o, i in pairs], r, w, (len(pairs), 1.0), "d", nbytes)

    def send(name, to_rank, from_rank, out, in_, r, w, nbytes):
        dst, src, sem = T.cores[to_rank % N], T.cores[from_rank % N], "r" + name
        engines = topo.engines(core, dst)
        if name in RELAYED:
            dst, src, sem = helper_of(core, T, topo), helper_of(src, T, topo), "h" + name
            engines = [e for e in topo.engines(core, dst) if e not in engines]
        rid, pid, _se = topo.addr(dst)

        def fn():
            g.remote_dma(out, in_, T.sem[sem], T.sem.loc, pid, rid, sum(1 << e for e in engines))
            return []
        add("s" + name, "g", fn, r, ["sent" + name], (1, 1.0), "s", (nbytes, len(engines)))
        add("r" + name, None, None, ["sent" + name], w, (0, 0.0), "r", len(topo.engines(src, core)))

    def col(j):
        return T.C[:, j:j + 1]

    def wide(h):
        return slice(H * h, H * h + H)

    def wr(h, o=0):
        return slice(o + 32 * h, o + 32 * h + 32)

    def cells(bank, c0, n):
        return ["%s:%d" % (bank, c) for c in range(c0 // 32, (c0 + n) // 32)]

    def extract(name, bank, weights, src, o, n, r, c0=0, more=()):
        out = T[bank][:, c0:c0 + n // 16]
        grp = [(out, l, x) for l, x in more] + [(out, weights[:, 15 - a:143 - a], src[:, o + a:o + n:16]) for a in range(16)]
        mm(name, grp, r, cells(bank, c0, n // 16), len(grp) * 64)

    def small(fn, *a):
        return lambda: fn(*a, allow_small_or_imprecise_dtypes=True)

    AK = ["A%d" % i for i in range(W // H)]
    PK = ["PTs", "PT00", "PT01", "PT10", "PT11"]

    def ak(i):
        return AK[i * len(AK) // NCH:(i + 1) * len(AK) // NCH]

    dma("lp", "s", [(T.DEN[:, 0:384], T.par[:]), (T.DEN[0:112, 384:512], T.mnt[1:8, :]),
                    (T.DEN[112:128, 384:512], T.mnt[0:1, :])], [], ["DEN"], 262144)
    dma("le", "s", [(T.EI[:], T.e0[:]), (T.NI[:], T.ns0[:])], [], ["EI", "NI"], 65536)
    dma("lu", "s", [(T.UK[:], T.u0[:])], [], ["UK"], 32768)
    add("fill0", "v", lambda: [V.memset(T.PT[:, 0:K], 0.0)], [], ["PTa"], (K, 0.5))
    add("ones", "v", lambda: [V.memset(T.ONES[:], 1.0)], [], ["ONES"], (576, 0.5))
    add("fill1", "v", lambda: [V.memset(T.PT[:, K:BASE], 0.0)], [], ["PTb"], (BASE - K, 0.5))
    for t in range(2):
        act("fill%d" % (2 + t), T.PT[:, BASE + K * t:BASE + K * t + K], T.PT[:, 0:K], ACT.Copy, 0.0, 1.0, ["PTa"],
            ["PT%d0" % t, "PT%d1" % t], K)
    cp("dhi", T.DHI[:], T.DEN[:], ["DEN"], ["DHI"], 512)
    tt("dlo", T.DLO[:], T.DEN[:], T.DHI[:], ALU.subtract, ["DEN", "DHI"], ["DLO"], 512, 2)
    cp("ub", T.UB[:], T.UK[:], ["UK"], ["UB"], 64)
    dma("lu8", "s", [(T.U8[:], T.UB[:])], ["UB"], ["U8"], 16384)
    dma("lpt", "s", [(T.PT[0:128:16, :], T.DHI[:, 0:384]), (T.PT[1:128:16, :], T.DLO[:, 0:384]),
                     (T.PT[14:128:16, 0:E], T.DHI[:, 384:512]), (T.PT[15:128:16, 0:E], T.DLO[:, 384:512])],
        ["DHI", "DLO"], PK + ["PTa", "PTb"], 262144)
    cw = W // NCH
    for i in range(NCH):
        dma("li%d" % i, OPT["lq"][i], [(T.A[:, cw * i:cw * i + cw], T.idm[:, cw * i:cw * i + cw])], [], ak(i), 256 * cw)
    dma("lac", "s", [(T.AC[0:112, :], T.ac[16:128, :]), (T.AC[112:128, :], T.ac[0:16, :])], [], ["AC"], 4 * 128 * E)
    send("e00", rank + 1, rank - 1, T.ERI[:], T.EI[:], ["EI"], ["ERI"], 32768)
    cp("er0", T.ER[:, 0:64], T.ERI[:], ["ERI"], ["ER00", "ER01"], 64)
    for i in range(NCH):
        a = T.A[:, cw * i:cw * i + cw]
        if OPT["cv"][i] == "a":
            act("cv%d" % i, a, a, ACT.Identity, 1.0 / 64, 1.0 / 32, ak(i), ak(i), cw)
        else:
            ts("cv%d" % i, a, a, 0.5, 1.0 / 32, ALU.add, ALU.mult, ak(i), ak(i), cw, 0.5)
    cp("nu0", T.NU[:], T.NI[:], ["NI"], ["NU0", "NU1"], 64)
    cp("ns0", T.NS[:], T.NI[:], ["NI"], ["NS"], 64)
    for t in range(2):
        s0 = BASE + K * t
        dma("old%d" % t, "s", [(T.WIN[:, 2 * K * t + K * h + H:2 * K * t + K * h + K], T.A[:, s0 + H * h:s0 + H * h + H]) for h in range(2)],
            AK[s0 // H:s0 // H + 2], ["OLD_%d0" % t, "OLD_%d1" % t], 256 * K)

    gop("iki", lambda: g.iota(T.KI[:, 0:1], [[0, 1]], 0, 1), [], ["KI0"], 1)
    gop("ixx", small(g.iota, T.XX[:], [[0, 2], [1, 128]], 0, 0), [], ["XX"], 256)
    gop("ixb", small(g.iota, T.XB[:], [[0, 2], [16, 8], [0, 16]], 0, 0), [], ["XB"], 256)
    gop("iiw", small(g.iota, T.IWR[:], [[0, 2], [16, 32]], H, 1), [], ["IWR"], 64)
    gop("ick", small(g.iota, col(CK), [[0, 1]], 0, 1), [], ["ck"], 1)
    gop("isg", small(g.iota, T.SG[:], [[0, 8], [-4096, 16]], 8192, 0), [], ["SG"], 128)
    gop("sel", lambda: g.affine_select(T.SEL[:], T.ONES[0:8, 0:128], [[-1, 8], [0, 16]], ALU.is_equal, 0.0, 0, 1), ["ONES"], ["SEL"], 128)
    gop("idw", lambda: g.affine_select(T.IDW[:], T.ONES[:, 0:132], [[-1, 132]], ALU.is_equal, 0.0, 3, 1), ["ONES"], ["IDW"], 132)
    for q in range(4):
        gop("ma%d" % q, lambda q=q: g.affine_select(T.MA[:, 576 * q:576 * q + 576], T.ONES[:], [[-1, 4], [-16, 9], [1000, 16]],
                                                    ALU.is_equal, 0.0, -1000 - 4 * q, 1), ["ONES"], ["MA%d" % q], 576)
    ts("kg", T.KI[:, 4:5], T.KI[:, 0:1], 112, None, ALU.bitwise_and, None, ["KI0"], ["KI1"], 1)
    ts("kr", T.KI[:, 5:6], T.KI[:, 0:1], 15, None, ALU.bitwise_and, None, ["KI0"], ["KI2"], 1)
    cp("cr", T.C[:, CG16:CG16 + 2], T.KI[:, 4:6], ["KI1", "KI2"], ["cr", "cg"], 1)
    for nm, j, b, s in (("cbu", CBU, 0.0, -2.0), ("cb1", CB1, -1.0, -2.0), ("cb961", CB961, -961.0, -2.0),
                        ("ckt", CKT, 20.0, 1.0), ("crh", CRH, 0.0, 0.5)):
        act(nm, col(j), col(CR), ACT.Identity, b, s, ["cr"], [nm], 1)
    ts("cm14", col(CM14), col(CR), 13.5, None, ALU.is_ge, None, ["cr"], ["cm14"], 1)
    ts("cw1", col(CW1), col(CR), 2.0, -2.0, ALU.is_equal, ALU.mult, ["cr"], ["cw1"], 1)
    ts("cw", col(CW), col(CR), 4.5, col(CW1), ALU.is_lt, ALU.add, ["cr", "cw1"], ["cw"], 1)
    ts("cq1", col(CQ1), col(CR), -3.0, col(CR), ALU.add, ALU.mult, ["cr"], ["cq1"], 1)
    ts("cq2", col(CQ2), col(CQ1), 0.0, 16.0, ALU.not_equal, ALU.mult, ["cq1"], ["cq2"], 1)
    ts("cq3", col(CQ3), col(CR), -2.0, 0.0, ALU.add, ALU.min, ["cr"], ["cq3"], 1)
    ts("cbp", col(CBP), col(CQ3), 8192.0, col(CQ2), ALU.mult, ALU.add, ["cq3", "cq2"], ["cbp"], 1)
    ts("y", T.Y[:], T.XB[:], col(CG16), None, ALU.is_equal, None, ["XB", "cg"], ["Y"], 256, 0.5)
    act("yn", T.YN[:], T.Y[:], ACT.Copy, 0.0, -1.0, ["Y"], ["YN"], 256)
    act("wz2", T.WZ2[:], T.Y[:, 16:144], ACT.Copy, 0.0, 2.0, ["Y"], ["WZ2"], 128)
    own, nxt, prv = T.XX[:, 113:256], T.XX[:, 97:240], T.XX[:, 1:144]
    for nm, src, wt, wk in (("EP", own, col(CW), "cw"), ("EM", nxt, col(CM14), "cm14"), ("EV", prv, 2047.0, "cg"),
                            ("EF", prv, -float(H), "cg"), ("EK", prv, col(CKT), "ckt"), ("EO", own, col(CRH), "crh")):
        ts(nm.lower(), T[nm][:, 0:143], src, col(CG16), wt, ALU.is_equal, ALU.mult, ["XX", "cg", wk], [nm], 143, 0.5)
    ts("sh", T.SH[:], T.XX[:, 112:240], col(CK), None, ALU.is_equal, None, ["XX", "ck"], ["SH"], 128, 0.5)
    gop("wz1", lambda: g.affine_select(T.WZ1[:], T.WZ2[:], [[1, 128]], ALU.not_equal, -62.0, 16, -1), ["WZ2"], ["WZ1"], 128)
    gop("wz", lambda: g.affine_select(T.WZ[:], T.WZ1[:], [[1, 128]], ALU.not_equal, -62.0, -112, -1), ["WZ1"], ["WZ"], 128)
    tt("wp", T.WP[:], T.SG[:], T.WZ2[:], ALU.mult, ["SG", "WZ2"], ["WP"], 128, 2)
    ts("iw", T.IW[:], T.IWR[:], col(CG16), None, ALU.subtract, None, ["IWR", "cg"], ["IW"], 32)

    for h in range(2):
        mm("pu%d" % h, [(T["S%d" % h][:], T.SEL[:], T.U8[:, wide(h)])], ["SEL", "U8"], ["S%d" % h], H)
        act("z0i%d" % h, T.Z0[:, wide(h)], T["S%d" % h][:], ACT.Abs, col(CBU), 2.0, ["cbu"], ["S%d" % h, "Z0%d" % h], H)

    def lookup(name, parts, banks, c0, weights, wk, src, sk, dst, dk, more=None):
        for j in range(parts):
            hs = [j] if parts == 2 else [0, 1]
            n, nm, bank = H * len(hs), "%s%d" % (name, j), banks[j]
            c = slice(32 * hs[0], 32 * hs[0] + 32 * len(hs))
            got, gk = T[bank][:, c0 + c.start:c0 + c.stop], cells(bank, c0 + c.start, n // 16)
            extract("x" + nm, bank, weights, src, H * hs[0], n, [wk] + [sk + str(h) for h in hs], c0 + c.start)
            cp("u" + nm, dst[:, c], got, gk, [dk + str(h) for h in hs], 64)
            if more is not None:
                act("s" + nm, T.UPS[:, c], got, ACT.Identity, more, 1.0, gk, ["UPS%d" % h for h in hs], 64)

    def parts(kind, t, h):
        return [[h]] if OPT[kind][t] == "2" else [[0, 1]] if h == 1 else []

    same, up1, nsame, nup1 = T.Y[:, 0:128], T.Y[:, 112:240], T.YN[:, 0:128], T.YN[:, 112:240]
    for t in range(RO):
        S0 = BASE + K * (t % 2)
        last = t == RO - 1
        n_ = lambda s, h=None, t=t: "%s_%d" % (s, t) if h is None else "%s_%d%d" % (s, t, h)
        eng = lambda s, h, t=t: OPT[s][2 * t + h]
        wino = 2 * K * t
        for h in range(2):
            er, erk = T.ER[:, wr(h, 64 * t)], "ER%d%d" % (t, h)
            pick(eng("mg", h), n_("mg", h), T.MG[:, wide(h)], T.PT[:, 0:E].indirect(er), ["PTs", erk], ["MG%d" % h])
        lookup(n_("m"), int(OPT["xm"][t]), ("X1", "X1"), 0, T.EM, "EM", T.MG, "MG", T.MU, "MU")
        for h in range(2):
            er, erk = T.ER[:, wr(h, 64 * t)], "ER%d%d" % (t, h)
            o = K * t + H * h
            pick(eng("cg", h), n_("cg", h), T.CS[:, o:o + H], T.A[:].indirect(T.MU[:, wr(h)]), AK + ["MU%d" % h], [n_("CS", h)])
            send("c%d%d" % (t, h), rank - 1 - t, rank + 1 + t, T.CL[:, o:o + H], T.CS[:, o:o + H], [n_("CS", h)], [n_("CL", h)], 256 * H)
            ts(n_("ag", h), T.AS[:, o:o + H], T.AC[:].indirect(er), -1.0, float(E), ALU.mult, ALU.add, ["AC", erk], [n_("AS", h)], H, "gather")
            send("a%d%d" % (t, h), rank - 1 - t, rank + 1 + t, T.AL[:, o:o + H], T.AS[:, o:o + H], [n_("AS", h)], [n_("AL", h)], 256 * H)
        for h in range(2):
            pick(eng("pg0", h), n_("pg0", h), T.PG[:, wide(h)], T.PT[:].indirect(T.NU[:, wr(h)]), PK + ["NU%d" % h], ["PG%d" % h])
        lookup(n_("n1"), int(OPT["x1"][t]), *OPT["n1"], T.EP, "EP", T.PG, "PG", T.N1U, "N1U", float(-S0))
        for h in range(2):
            pick(eng("pg1", h), n_("pg1", h), T.PG2[:, wide(h)], T.PT[:].indirect(T.N1U[:, wr(h)]), PK + ["N1U%d" % h], ["PG2%d" % h])
        lookup(n_("n2"), int(OPT["x2"][t]), *OPT["n2"], T.EP, "EP", T.PG2, "PG2", T.N2U, "N2U")
        if not last:
            act(n_("ph"), T.PH[:], T.NS[:], ACT.Copy, 0.0, 1.0, ["NS"], ["PH"], 64)
            tt(n_("pl"), T.PL[:], T.NS[:], T.PH[:], ALU.subtract, ["NS", "PH"], ["PL"], 64, 2)
            for h in range(2):
                zb = "ZB%d" % h
                for j in range(4):
                    grp = [(T[zb][:], T.IDW[:, 0:128], T.PT[:, S0 + H * h:S0 + H * h + H])] if j == 0 else []
                    for a in range(4 * j, 4 * j + 4):
                        grp += [(T[zb][:, a:H:16], T.MA[:, 144 * a + 1:144 * a + 129], T.PH[:, wr(h)]),
                                (T[zb][:, a:H:16], T.MA[:, 144 * a:144 * a + 128], T.PL[:, wr(h)])]
                    mm(n_("pp%d" % j, h), grp, ["IDW", "PT%d%d" % (t, h), "MA%d" % j, "PH", "PL"], [zb], 512 + (H if j == 0 else 0),
                       j == 0, False)
        else:
            mm("xu", [(T.ZB0[:, 0:64], T.EO[:, 15 - a:143 - a], T.Z0[:, 64 * a:64 * a + 64]) for a in range(16)],
               ["EO", "Z00", "Z01"], ["ZB0"], 1024)
            act("uo", T.UO[:], T.ZB0[:, 0:64], ACT.Identity, -40.0, 1.0, [], ["ZB0", "UO"], 64)
        for h in range(2):
            sbk, zb, ab = "S%d" % h, "ZB%d" % h, "AB%d" % h
            lists = (("NU", T.NU), ("N1U", T.N1U), ("N2U", T.N2U))
            marks = (("Z0", T.Z0), ("Z1", T.Z1), ("Z2", T.Z2))
            tk, ttv = "TT%d" % h, T.TT[:, wide(h)]
            by_act = eng("hit", h) == "a"
            for s in range(3):
                zk, z = marks[s][0] + str(h), marks[s][1][:, wide(h)]
                column, ck = T.A[:].indirect(lists[s][1][:, wr(h)]), AK + [lists[s][0] + str(h)]
                if eng("g%d" % s, h) == "f":
                    tt(n_("g%d" % s, h), ttv, column, z, ALU.max, ck + [zk], [tk], H, "gather2")
                else:
                    gc, gk = T.GC[:, K * s + H * h:K * s + H * h + H], "GC%d%d" % (s, h)
                    pick(eng("g%d" % s, h), n_("gc%d" % s, h), gc, column, ck, [gk])
                    mm(n_("pm%d" % s, h), [(T[ab][:], T.IDW[:, 3:131], z)], ["IDW", zk], [ab], H)
                    tt(n_("g%d" % s, h), ttv, T[ab][:], gc, ALU.max, [gk], [ab, tk], H)
                pos, neg = (same, nsame) if s < 2 else (nup1, up1) if by_act else (up1, nup1)
                opens = True
                if s > 0 or t == 0:
                    mm(n_("pn%d" % s, h), [(T[sbk][:], neg, z)], ["Y", "YN", zk], [sbk], H, True, False)
                    opens = False
                mm(n_("ps%d" % s, h), [(T[sbk][:], pos, ttv)], ["Y", "YN", tk], [sbk], H, opens, not (s == 2 and by_act))
                if s < 2:
                    bk, b = ("cb961", CB961) if (s == 0 and t > 0) else ("cb1", CB1)
                    act(n_("z%d" % (s + 1), h), marks[s + 1][1][:, wide(h)], T[sbk][:], ACT.Abs, col(b), 64.0,
                        [bk], [sbk, marks[s + 1][0] + str(h)], H)
            o = K * t + H * h
            hk, hv = "HIT%d" % h, T.HIT[:, wide(h)]
            if by_act:
                mm(n_("pc", h), [(T[sbk][:], T.IDW[:, 3:131], T.CL[:, o:o + H])], ["IDW", n_("CL", h)], [sbk], H, False, True)
                act(n_("far", h), T.Z1[:, wide(h)], T[sbk][:], ACT.Abs, 0.0, 64.0, [], [sbk, "Z1%d" % h], H)
                act(n_("hit", h), hv, T.Z1[:, wide(h)], ACT.Relu, 1.0, -1.0, ["Z1%d" % h], [hk], H)
            else:
                tt(n_("hit", h), hv, T[sbk][:], T.CL[:, o:o + H], ALU.is_equal, [n_("CL", h)], [sbk, hk], H)
            mm(n_("pa", h), [(T[ab][:], T.SH[:], T.AL[:, o:o + H])], ["SH", n_("AL", h)], [ab], H)
            tt(n_("val", h), T.VAL[:, wide(h)], T[ab][:], hv, ALU.mult, [hk], [ab, "VAL%d" % h], H)
            for hs in ([] if last else parts("xf", t, h)):
                c, n = slice(32 * hs[0], 32 * hs[-1] + 32), 32 * len(hs)
                extract(n_("xf", h), "X1", T.EF, T.HIT, H * hs[0], 16 * n, ["EF", "SH", "IW"] + ["HIT%d" % j for j in hs], 64 + c.start,
                        [(T.SH[:], T.IW[:, 0:n])])
                cp(n_("ou", h), T.OU[:, c], T.X1[:, 64 + c.start:64 + c.stop], cells("X1", 64 + c.start, n), ["OU%d" % j for j in hs], n)
            for hs in parts("xv", t, h):
                extract(n_("xv", h), "X0", T.EV, T.VAL, H * hs[0], H * len(hs), ["EV"] + ["VAL%d" % j for j in hs], 32 * hs[0])
            if not last:
                dma("sh%d%d" % (t, h), "s", [(T.WIN[0:112, wino + K * h:wino + K * h + H], T.CL[16:128, o:o + H]),
                                             (T.WIN[112:128, wino + K * h:wino + K * h + H], T.CL[0:16, o:o + H])],
                    [n_("CL", h)], [n_("NEW", h)], 256 * H)
                mm(n_("pq", h), [(T[zb][:], T.WP[:], hv)], ["WP", hk], [zb], H, False, True)
                mm(n_("py", h), [(T[sbk][:], T.IDW[:, 3:131], T.Z0[:, wide(h)])], ["IDW", "Z0%d" % h], [sbk], H, True, False)
                mm(n_("pz", h), [(T[sbk][:], T.WZ[:], hv)], ["WZ", hk], [sbk], H, False, True)
                act(n_("z0", h), T.Z0[:, wide(h)], T[sbk][:], ACT.Sign, -0.5, 1.0, [], [sbk, "Z0%d" % h], H)
            for hs in parts("xv", t, h):
                c = slice(32 * hs[0], 32 * hs[-1] + 32)
                k_ = lambda s, hs=hs: [s + str(j) for j in hs]
                old, ok_ = (T.EI, ["EI"]) if t == 0 else (T.EN, k_("EN"))
                tt(n_("ey", h), T.EY[:, c], T.X0[:, c], old[:, c], ALU.max, ok_ + k_("X0:"), k_("EY"), 32)
                ts(n_("en", h), T.EN[:, c], T.EY[:, c], E - 1, None, ALU.bitwise_and, None, k_("EY"), k_("EN"), 32)
                if last:
                    cp("ew", T.EW[:], T.EN[:], k_("EN"), ["EW"], 64)
                    continue
                euk, ce = "EU%d%d" % (t + 1, h), slice(64 * t + 64 + c.start, 64 * t + 64 + c.stop)
                cp(n_("eu", h), T.EU[:, ce], T.EN[:, c], k_("EN"), [euk], 32)
                send("e%d%d" % (t + 1, h), rank + 2 + t, rank - 2 - t, T.ER[:, ce], T.EU[:, ce], [euk], k_("ER%d" % (t + 1)), 8192 * len(hs))
        if last:
            ts(n_("nok"), T.NOK[:], T.X0[:, 0:64], 0.0, None, ALU.is_equal, None, cells("X0", 0, 64), ["NOK"], 64)
        else:
            ts(n_("nok"), T.NOK[:], T.X1[:, 64:128], float(H), None, ALU.is_ge, None, cells("X1", 64, 64), ["NOK"], 64)
        tt(n_("tn"), T.TN[:], T.NOK[:], T.UPS[:], ALU.mult, ["NOK", "UPS0", "UPS1"], ["TN"], 64, 2)
        cp(n_("xi"), T.XI[:], T.X0[:, 0:64], cells("X0", 0, 64), ["XI"], 64)
        ts(n_("xl"), T.XL[:], T.XI[:], K - 1, None, ALU.bitwise_and, None, ["XI"], ["XL"], 64)
        tt(n_("td"), T.TD[:], T.XL[:], T.TN[:], ALU.add, ["XL", "TN"], ["TD"], 64, 2)
        if not last:
            ts(n_("nu"), T.NU[:], T.TD[:], float(S0), None, ALU.add, None, ["TD"], ["NU0", "NU1"], 64)
        if t != 1:
            act(n_("ns"), T.NS[:], T.TD[:], ACT.Identity, float(S0), 1.0, ["TD"], ["NS"], 64)
        if last:
            mm("xk", [(T.ZB1[:, 0:64], T.EK[:, 15 - a:143 - a], T.HIT[:, 64 * a:64 * a + 64]) for a in range(16)],
               ["EK", "HIT0", "HIT1"], ["ZB1"], 1024)
            tt("uj", T.UJ[:], T.ZB1[:, 0:64], T.UO[:], ALU.max, ["UO"], ["ZB1", "UJ"], 64)
            act("uf", T.UF[:], T.UJ[:], ACT.Abs, -20.0, 1.0, ["UJ"], ["UF"], 64)
        else:
            for h in range(2):
                zb, ao = "ZB%d" % h, S0 + H * h
                pick(eng("ins", h), n_("ins", h), T.A[:, ao:ao + H], T.WIN[:, wino + K * h:wino + K * h + K].indirect(T.OU[:, wr(h)]),
                     [n_("OLD", h), n_("NEW", h), "OU%d" % h], ["A%d" % (ao // H)])
                act(n_("pe", h), T.PT[:, ao:ao + H], T[zb][:], ACT.Relu, col(CBP), 1.0, ["cbp"], [zb, "PT%d%d" % (t, h)], H)
    dma("ou", "a", [(T.yu[:], T.UF[:])], ["UF"], [], 32768)
    dma("oe", "s", [(T.ye[:], T.EW[:])], ["EW"], [], 32768)
    dma("on", "a", [(T.yn[:], T.NS[:])], ["NS"], [], 32768)
    return ops


def deps_of(ops):
    def pieces(keys):
        return [p for k in keys for p in (["%s:%d" % (k, c) for c in range(6)] if k in BANKS else [k])]

    lw, rd, out = {}, {}, []
    for i, o in enumerate(ops):
        look = [k for k in o["w"] if k in BANKS and o["q"] != "p"]
        reads, writes = pieces(o["r"] + look), pieces([k for k in o["w"] if k not in look])
        d = set(lw[k] for k in reads + writes if k in lw)
        for k in writes:
            d.update(rd.get(k, []))
        d.discard(i)
        out.append(sorted(d))
        for k in reads:
            rd.setdefault(k, []).append(i)
        for k in writes:
            lw[k] = i
            rd[k] = []
    return out


def banks_of(o):
    return sorted(set(k.split(":")[0] for k in o["r"] + o["w"]) & set(BANKS))


def in_turns(ops, deps, seq):
    out, last = [list(d) for d in deps], {}
    for i in seq:
        for b in banks_of(ops[i]):
            seen = last.setdefault(b, {})
            out[i] += [j for q, j in seen.items() if q != ops[i]["q"]]
            seen[ops[i]["q"]] = i
    return out


ORDER = """
lu le li0 lp fill0 ixb ixx iki fill2 fill3 fill1 ones kr kg ns0 cr ub y cm14 cw1 dhi dlo nu0 li1 li3 lu8 li2 li5 se00
li4 sel ick ma0 idw lpt lac pu1 pu0 cv0 cbu ph_0 ckt yn cv1 cb1 z0i1 wz2 z0i0 cv2 pg0_01 pg0_00 cv3 pl_0 cw cq1 em cv5
ep er0 cv4 cq2 ef sh mg_00 pn0_01 pp0_00 pn0_00 xm_00 pp0_01 xn1_01 xn1_00 g0_01 um_00 cq3 g0_00 un1_01 un1_00 cbp ag_00
cg_00 mg_01 iiw ma1 ma2 isg ma3 wz1 sc00 sa00 old0 ps0_00 pp1_01 pp2_01 xm_01 pp1_00 ps0_01 z1_00 pg1_01 g1_00 ag_01
z1_01 pg1_00 xn2_01 pn1_00 pn1_01 ps1_00 um_01 g1_01 xn2_00 z2_00 un2_00 ek g2_00 wp ev pp2_00 pp3_01 pn2_00 ps1_01
pp3_00 cg_01 sn1_00 z2_01 sn1_01 sa01 sc01 wz sh00 ps2_00 pn2_01 pa_00 hit_00 un2_01 iw g2_01 pq_00 xf_00 pa_01 py_00
sh01 ps2_01 pz_00 ou_00 val_00 hit_01 xv_00 ey_00 val_01 en_00 pq_01 xf_01 eu_00 ou_01 nok_0 xv_01 pe_00 cb961 ins_00
z0_00 crh pe_01 ins_01 se10 py_01 tn_0 xi_0 ey_01 xl_0 en_01 td_0 eu_01 nu_0 pg0_11 g0_10 pz_01 ns_0 z0_01 pg0_10 mg_10
ph_1 xn1_10 xm_10 ps0_10 ag_10 pl_1 un1_10 um_10 g0_11 se11 mg_11 cg_10 z1_10 pp0_10 xm_11 pp0_11 ps0_11 pp1_11 pg1_10
ag_11 um_11 g1_10 z1_11 cg_11 xn2_10 pn1_10 pn1_11 ps1_10 un2_10 g1_11 sa10 old1 sc10 sa11 sc11 sh10 pp1_10 pa_10 z2_10
pp2_10 pn2_10 ps1_11 pp2_11 g2_10 pg1_11 z2_11 ps2_10 xn2_11 hit_10 un2_11 val_10 g2_11 pp3_11 py_10 pn2_11 xv_10 sn1_10
pa_11 pz_10 ey_10 z0_10 ps2_11 en_10 eu_10 xf_10 hit_11 se20 sh11 ou_10 val_11 xf_11 ins_10 xv_11 nok_1 eo tn_1 ou_11
ey_11 xi_1 en_11 xl_1 eu_11 td_1 ins_11 ag_20 nu_1 pq_11 pp3_10 py_11 pz_11 pq_10 pe_11 mg_20 pe_10 z0_11 se21 xm_20
um_20 sa20 g0_20 g0_21 pg0_20 cg_20 mg_21 ps0_20 xu xm_21 sc20 pg0_21 z1_20 um_21 xn1_20 ps0_21 pn1_20 cg_21 ag_21
un1_20 g1_20 sc21 sa21 z1_21 pg1_20 g1_21 ps1_20 xn2_20 pa_20 pn1_21 z2_20 pg1_21 un2_20 g2_20 ps1_21 xn2_21 un2_21
sn1_20 z2_21 uo g2_21 pn2_20 pn2_21 ps2_20 ps2_21 hit_20 pa_21 hit_21 val_20 xk val_21 xv_21 uj nok_2 xi_2 tn_2 ey_21
xl_2 en_21 td_2 ew uf ou oe ns_2 on
"""


def plan(ops, deps):
    index = {o["name"]: i for i, o in enumerate(ops)}
    seq = []
    for s in ORDER.split():
        seq.append(index[s])
        if ops[index[s]]["kind"] == "s":
            seq.append(index["r" + s[1:]])
    assert sorted(seq) == list(range(len(ops)))
    place = {j: p for p, j in enumerate(seq)}
    assert all(place[d] < place[i] for i in seq for d in deps[i])
    return seq


def helper_of(core, T, topo):
    return [c for c in topo.cores_of(core) if T.rank_of(c) is None and topo.die(c) == topo.die(core)
            and topo.addr(c)[2] != topo.addr(core)[2]][0]


def helper_program(g, core, owner, T, topo):
    sent = 0
    for name in RELAYED:
        t, h = int(name[1]), int(name[2])
        dst = T.cores[(T.rank_of(owner) - 1 - t) % N]
        rid, pid, _se = topo.addr(dst)
        piece = T.AL[:, K * t + H * h:K * t + H * h + H]
        g.wait_ge(T.sem["h" + name], len(topo.engines(owner, core)) - len(topo.engines(owner, dst)))
        g.remote_dma(piece, piece, T.sem["r" + name], T.sem.loc, pid, rid, topo.mask(core, dst))
        sent += len(topo.engines(core, dst))
    g.wait_ge(T.sem.loc, sent)


def rank_program(g, core, T, topo):
    if T.rank_of(core) is None:
        for owner in T.cores:
            if helper_of(owner, T, topo) == core:
                helper_program(g, core, owner, T, topo)
        return
    ops = build_ops(g, T, topo, core)
    deps = deps_of(ops)
    seq = plan(ops, deps)
    deps = in_turns(ops, deps, seq)
    queue = {"v": g.vector, "a": g.scalar, "p": g.tensor, "g": g, "s": g.sync}
    csem = {"v": "cv", "a": "ca", "p": "cp", "g": "cg"}
    known = {q: {} for q in queue}
    total = {}
    mark = {}
    for i in seq:
        o = ops[i]
        q = o["q"]
        if o["kind"] == "r":
            total[o["name"]] = o["x"]
            mark[i] = (o["name"], o["x"], {})
            continue
        kn = known[q]
        need = [mark[d] for d in deps[i] if d in mark and not (q == "p" and ops[d]["q"] == "p")]
        for s, v, clock in sorted(need, key=lambda m: -m[1]):
            if kn.get(s, 0) >= v:
                continue
            queue[q].wait_ge(T.sem[s], v)
            kn[s] = v
            for s2, v2 in clock.items():
                kn[s2] = max(kn.get(s2, 0), v2)
        ins = o["fn"]()
        if o["kind"] == "s":
            total["loc"] = total.get("loc", 0) + o["x"][1]
            continue
        s, step = (o["name"], 16) if o["kind"] == "d" else (csem[q], 1)
        for x in ins:
            x.then_inc(T.sem[s], step)
            total[s] = total.get(s, 0) + step
        mark[i] = (s, total[s], dict(kn))
    for s, v in total.items():
        if max(known[q].get(s, 0) for q in queue) < v:
            g.wait_ge(T.sem[s], v)
